import numpy as np
import ml_dtypes


def mxq(x, axis, fmt="e4m3"):
    dtype, down = {"e4m3": (ml_dtypes.float8_e4m3fn, 7), "e5m2": (ml_dtypes.float8_e5m2, 14)}[fmt]
    v = np.moveaxis(np.asarray(x, np.float32).astype(ml_dtypes.bfloat16).astype(np.float64), axis, -1)
    blocks = v.reshape(v.shape[:-1] + (-1, 32))
    amax = np.abs(blocks).max(-1, keepdims=True)
    byte = np.maximum(np.where(amax > 0, np.frexp(amax)[1] - 1 + 127, 0) - down, 1)
    scale = np.exp2(byte - 127.0)
    codes = (blocks / scale).astype(np.float32).astype(dtype).astype(np.float64)
    return np.moveaxis((codes * scale).reshape(v.shape), -1, axis)


WIDE = False


def mx_kscale(k):
    if not WIDE:
        return np.ones(k)
    levels = np.array([10, -10, 5, -5, 0])
    if k % 512:
        return np.exp2(np.random.permutation(np.resize(levels, k // 32))).repeat(32)
    a = np.empty((k // 512, 16))
    for p in range(k // 512):
        a[p, :8] = np.random.permutation(np.resize(levels, 8))
        for g in range(8):
            far = levels[np.abs(levels - a[p, g]) >= 10]
            a[p, g + 8] = far[np.random.randint(len(far))]
    return np.exp2(a.ravel()).repeat(32)


def f64(x):
    return np.asarray(x).astype(np.float64)


def striped(idx):
    return np.tile(idx.reshape(-1, 16).T, (8, 1)).astype(np.uint16)


def unstriped(offs):
    return offs[:16].T.reshape(-1).astype(np.int64)


def pack_weight(w):
    k, n = w.shape
    w = f64(np.asarray(w, np.float32).astype(ml_dtypes.bfloat16)).reshape(k // 32, 32, n)
    amax = np.abs(w).max(1)
    byte = np.clip(np.where(amax > 0, np.frexp(amax)[1] - 1 + 127 - 7, 1), 1, 254)
    scaled = (w * np.exp2(127.0 - byte)[:, None, :]).reshape(k, n).astype(np.float32)
    words = np.ascontiguousarray(scaled.reshape(k // 512, 128, 4, n).transpose(0, 1, 3, 2)).astype(ml_dtypes.float8_e4m3fn).view(np.uint8)
    return words, np.ascontiguousarray(byte.astype(np.uint8).reshape(k // 512, 16, n))


def unpack_weight(words, scales):
    g, p, n, _ = words.shape
    vals = np.ascontiguousarray(words).view(ml_dtypes.float8_e4m3fn).astype(np.float64) * np.repeat(np.exp2(scales.astype(np.float64) - 127.0), 8, axis=1)[..., None]
    return vals.transpose(0, 1, 3, 2).reshape(g * 512, n)


def gelu(v):
    return 0.5 * v * (1.0 + np.tanh(np.sqrt(2.0 / np.pi) * (v + 0.044715 * v**3)))


K, T, S, N = 512, 1024, 512, 128


def setup_inputs():
    n = np.random.standard_normal
    s = mx_kscale(K)[:, None]
    words, scales = pack_weight(n((K, N)) / np.sqrt(K) / s)
    return {
        "xT": (n((K, S)) * s).astype(np.float32),
        "w_words": words,
        "w_scales": scales,
        "b": (0.3 * n((N, 1))).astype(np.float32),
        "gate": np.tile(np.random.uniform(0.2, 1.0, S), (N, 1)).astype(np.float32),
        "offs": striped(np.random.permutation(T)[:S]),
    }


def reference(xT, w_words, w_scales, b, gate, offs):
    w = unpack_weight(w_words, w_scales)
    idx = unstriped(offs)
    xq = mxq(f64(xT), 0, "e4m3")
    y = w.T @ xq
    y = gelu(y + f64(b))
    out = np.zeros((N, T))
    out[:, idx] = f64(gate) * y
    return out

@@ -1,0 +1,127 @@
+from contextlib import ExitStack
+
+import concourse.mybir as mybir
+
+K, S, T, N = 512, 512, 1024, 128
+FLOPS = 2 * K * S * N
+
+F32 = mybir.dt.float32
+BF16 = mybir.dt.bfloat16
+I32 = mybir.dt.int32
+U32 = mybir.dt.uint32
+U16 = mybir.dt.uint16
+U8 = mybir.dt.uint8
+FP8X4 = mybir.dt.float8_e4m3fn_x4
+GELU = mybir.ActivationFunctionType.Gelu_apprx_tanh
+MULT = mybir.AluOpType.mult
+
+P = 128
+PACK = 4
+PIECE = 128
+LOADS = ((0, 256), (256, 512))
+
+
+def tile_picked_place_lin_gelu_sub_l_kernel(tc, xT, w_words, w_scales, b, gate, offs, out):
+    nc = tc.nc
+    with ExitStack() as ctx:
+        keep = ctx.enter_context(tc.tile_pool(name="keep", bufs=1))
+        psum = ctx.enter_context(tc.psum_pool(name="psum", bufs=1))
+
+        offsets = keep.tile([P, S // 16], U16, name="offsets")
+        w_codes = keep.tile([P, N], U32, name="w_codes", align_bytes=64)
+        w_plane = keep.tile([P, N], U8, name="w_plane", align_bytes=64)
+        bias = keep.tile([P, 1], F32, name="bias")
+        gates = keep.tile([P, S], F32, name="gates", align_bytes=64)
+        window = keep.tile([P, T], F32, name="window", align_bytes=64)
+        warm_in = keep.tile([P, 1], F32, name="warm_in")
+        warm_out = keep.tile([P, 1], F32, name="warm_out")
+
+        x_rows = xT.rearrange("(p j) w -> p j w", j=PACK)
+        raw = []
+        for lo, hi in LOADS:
+            t = keep.tile([P, PACK, hi - lo], F32, name=f"raw{lo}", align_bytes=64)
+            raw.append((lo, hi, t))
+
+        def load(queue, k):
+            lo, hi, t = raw[k]
+            queue.dma_start(out=t[:], in_=x_rows[:, :, lo:hi])
+
+        def load_scales(queue, q):
+            queue.dma_start(
+                out=w_plane[32 * q : 32 * q + 4, :].bitcast(I32),
+                in_=w_scales[0, 4 * q : 4 * q + 4, :].bitcast(I32),
+            )
+
+        load_scales(nc.sync, 0)
+        load_scales(nc.scalar, 1)
+        load(nc.sync, 0)
+        nc.scalar.dma_start(out=w_codes[:].bitcast(I32), in_=w_words[0].rearrange("p n t -> p (n t)").bitcast(I32))
+        load_scales(nc.sync, 2)
+        nc.scalar.dma_start(out=bias[:], in_=b)
+        load_scales(nc.sync, 3)
+        nc.gpsimd.dma_start(out=gates[:], in_=gate)
+        load(nc.sync, 1)
+        nc.sync.dma_start(offsets[:], offs)
+        nc.vector.memset(warm_in[:], 0.0)
+        nc.scalar.activation(warm_out[:], warm_in[:], GELU)
+        nc.vector.memset(window[:], 0.0)
+
+        grouped, codes, planes, acc, y = [], [], [], [], []
+        for i in range(S // PIECE):
+            grouped.append(keep.tile([P, PIECE, PACK], BF16, name=f"grouped{i}", align_bytes=64))
+            codes.append(keep.tile([P, PIECE], U32, name=f"codes{i}", align_bytes=64))
+            planes.append(keep.tile([P, PIECE], U8, name=f"planes{i}", align_bytes=64))
+            acc.append(psum.tile([N, PIECE], F32, name=f"acc{i}"))
+            y.append(keep.tile([N, PIECE], F32, name=f"y{i}", align_bytes=64))
+
+        def interleave(i, copy):
+            for lo, hi, t in raw:
+                if lo <= i * PIECE < hi:
+                    cols = slice(i * PIECE - lo, (i + 1) * PIECE - lo)
+                    copy(out=grouped[i][:], in_=t[:, :, cols].rearrange("p j w -> p w j"))
+
+        def quantise(i):
+            nc.vector.quantize_mx(
+                out=codes[i][:].bitcast(FP8X4),
+                scales=planes[i][:],
+                in_=grouped[i][:].rearrange("p w j -> p (w j)"),
+            )
+
+        def multiply(i):
+            nc.tensor.matmul_mx(
+                out=acc[i][:],
+                lhsT=w_codes[:].bitcast(FP8X4),
+                lhsT_scale=w_plane[:],
+                rhs=codes[i][:].bitcast(FP8X4),
+                rhs_scale=planes[i][:],
+                start=True,
+                stop=True,
+            )
+            nc.scalar.activation(y[i][:], acc[i][:], GELU, bias=bias[:])
+
+        def place(i):
+            cols = slice(i * PIECE // 16, (i + 1) * PIECE // 16)
+            nc.vector.tensor_tensor(
+                window[:].indirect(offsets[:, cols]),
+                y[i][:],
+                gates[:, i * PIECE : (i + 1) * PIECE],
+                MULT,
+            )
+
+        interleave(0, nc.vector.tensor_copy)
+        quantise(0)
+        multiply(0)
+        interleave(1, nc.scalar.copy)
+        quantise(1)
+        multiply(1)
+        interleave(2, nc.scalar.copy)
+        place(0)
+        quantise(2)
+        multiply(2)
+        interleave(3, nc.scalar.copy)
+        place(1)
+        quantise(3)
+        multiply(3)
+        place(2)
+        place(3)
+        nc.sync.dma_start(out=out, in_=window[:])

@@ -17,8 +17,9 @@ MULT = mybir.AluOpType.mult
 
 P = 128
 PACK = 4
-PIECE = 128
-LOADS = ((0, 256), (256, 512))
+BANKS = ((0, 128), (128, 384), (384, 512))
+X_LOADS = ((0, 128), (128, 384), (384, 512))
+GATE_LOADS = ((0, 128), (128, 512))
 
 
 def tile_picked_place_lin_gelu_sub_l_kernel(tc, xT, w_words, w_scales, b, gate, offs, out):
@@ -31,20 +32,21 @@ def tile_picked_place_lin_gelu_sub_l_kernel(tc, xT, w_words, w_scales, b, gate, 
         w_codes = keep.tile([P, N], U32, name="w_codes", align_bytes=64)
         w_plane = keep.tile([P, N], U8, name="w_plane", align_bytes=64)
         bias = keep.tile([P, 1], F32, name="bias")
-        gates = keep.tile([P, S], F32, name="gates", align_bytes=64)
         window = keep.tile([P, T], F32, name="window", align_bytes=64)
         warm_in = keep.tile([P, 1], F32, name="warm_in")
         warm_out = keep.tile([P, 1], F32, name="warm_out")
 
         x_rows = xT.rearrange("(p j) w -> p j w", j=PACK)
-        raw = []
-        for lo, hi in LOADS:
-            t = keep.tile([P, PACK, hi - lo], F32, name=f"raw{lo}", align_bytes=64)
-            raw.append((lo, hi, t))
+        raw = [keep.tile([P, PACK, hi - lo], F32, name=f"raw{lo}", align_bytes=64) for lo, hi in X_LOADS]
+        gates = [keep.tile([P, hi - lo], F32, name=f"gates{lo}", align_bytes=64) for lo, hi in GATE_LOADS]
 
-        def load(queue, k):
-            lo, hi, t = raw[k]
-            queue.dma_start(out=t[:], in_=x_rows[:, :, lo:hi])
+        def load_x(queue, k):
+            lo, hi = X_LOADS[k]
+            queue.dma_start(out=raw[k][:], in_=x_rows[:, :, lo:hi])
+
+        def load_gate(queue, k):
+            lo, hi = GATE_LOADS[k]
+            queue.dma_start(out=gates[k][:], in_=gate[:, lo:hi])
 
         def load_scales(queue, q):
             queue.dma_start(
@@ -52,76 +54,90 @@ def tile_picked_place_lin_gelu_sub_l_kernel(tc, xT, w_words, w_scales, b, gate, 
                 in_=w_scales[0, 4 * q : 4 * q + 4, :].bitcast(I32),
             )
 
-        load_scales(nc.sync, 0)
+        def load_w(queue):
+            queue.dma_start(out=w_codes[:].bitcast(I32), in_=w_words[0].rearrange("p n t -> p (n t)").bitcast(I32))
+
+        def held(loads, tiles, lo, hi):
+            for (a, z), t in zip(loads, tiles):
+                if a <= lo and hi <= z:
+                    return t, slice(lo - a, hi - a)
+            raise ValueError("no load holds these columns")
+
+        load_scales(nc.scalar, 0)
+        load_x(nc.sync, 0)
         load_scales(nc.scalar, 1)
-        load(nc.sync, 0)
-        nc.scalar.dma_start(out=w_codes[:].bitcast(I32), in_=w_words[0].rearrange("p n t -> p (n t)").bitcast(I32))
-        load_scales(nc.sync, 2)
-        nc.scalar.dma_start(out=bias[:], in_=b)
-        load_scales(nc.sync, 3)
-        nc.gpsimd.dma_start(out=gates[:], in_=gate)
-        load(nc.sync, 1)
+        load_x(nc.sync, 1)
+        load_scales(nc.scalar, 2)
+        load_x(nc.sync, 2)
+        load_scales(nc.scalar, 3)
+        load_w(nc.sync)
+        nc.gpsimd.dma_start(out=bias[:], in_=b)
         nc.sync.dma_start(offsets[:], offs)
+        load_gate(nc.sync, 0)
+        load_gate(nc.sync, 1)
         nc.vector.memset(warm_in[:], 0.0)
         nc.scalar.activation(warm_out[:], warm_in[:], GELU)
         nc.vector.memset(window[:], 0.0)
 
-        grouped, codes, planes, acc, y = [], [], [], [], []
-        for i in range(S // PIECE):
-            grouped.append(keep.tile([P, PIECE, PACK], BF16, name=f"grouped{i}", align_bytes=64))
-            codes.append(keep.tile([P, PIECE], U32, name=f"codes{i}", align_bytes=64))
-            planes.append(keep.tile([P, PIECE], U8, name=f"planes{i}", align_bytes=64))
-            acc.append(psum.tile([N, PIECE], F32, name=f"acc{i}"))
-            y.append(keep.tile([N, PIECE], F32, name=f"y{i}", align_bytes=64))
+        grouped = keep.tile([P, S * PACK], BF16, name="grouped", align_bytes=64)
+        codes = keep.tile([P, S], U32, name="codes", align_bytes=64)
+        plane = keep.tile([P, S], U8, name="plane", align_bytes=64)
+        y = keep.tile([N, S], F32, name="y", align_bytes=64)
+        acc = [psum.tile([N, hi - lo], F32, name=f"acc{lo}") for lo, hi in BANKS]
 
-        def interleave(i, copy):
-            for lo, hi, t in raw:
-                if lo <= i * PIECE < hi:
-                    cols = slice(i * PIECE - lo, (i + 1) * PIECE - lo)
-                    copy(out=grouped[i][:], in_=t[:, :, cols].rearrange("p j w -> p w j"))
-
-        def quantise(i):
-            nc.vector.quantize_mx(
-                out=codes[i][:].bitcast(FP8X4),
-                scales=planes[i][:],
-                in_=grouped[i][:].rearrange("p w j -> p (w j)"),
+        def interleave(copy, lo, hi):
+            t, cols = held(X_LOADS, raw, lo, hi)
+            copy(
+                out=grouped[:, PACK * lo : PACK * hi].rearrange("p (w j) -> p w j", j=PACK),
+                in_=t[:, :, cols].rearrange("p j w -> p w j"),
             )
 
-        def multiply(i):
+        def quantise(lo, hi):
+            nc.vector.quantize_mx(
+                out=codes[:, lo:hi].bitcast(FP8X4),
+                scales=plane[:, lo:hi],
+                in_=grouped[:, PACK * lo : PACK * hi],
+            )
+
+        def multiply(lo, hi):
+            t, cols = held(BANKS, acc, lo, hi)
             nc.tensor.matmul_mx(
-                out=acc[i][:],
+                out=t[:, cols],
                 lhsT=w_codes[:].bitcast(FP8X4),
                 lhsT_scale=w_plane[:],
-                rhs=codes[i][:].bitcast(FP8X4),
-                rhs_scale=planes[i][:],
+                rhs=codes[:, lo:hi].bitcast(FP8X4),
+                rhs_scale=plane[:, lo:hi],
                 start=True,
                 stop=True,
             )
-            nc.scalar.activation(y[i][:], acc[i][:], GELU, bias=bias[:])
 
-        def place(i):
-            cols = slice(i * PIECE // 16, (i + 1) * PIECE // 16)
+        def activate(lo, hi):
+            t, cols = held(BANKS, acc, lo, hi)
+            nc.scalar.activation(y[:, lo:hi], t[:, cols], GELU, bias=bias[:])
+
+        def place(lo, hi):
+            t, cols = held(GATE_LOADS, gates, lo, hi)
             nc.vector.tensor_tensor(
-                window[:].indirect(offsets[:, cols]),
-                y[i][:],
-                gates[:, i * PIECE : (i + 1) * PIECE],
+                window[:].indirect(offsets[:, lo // 16 : hi // 16]),
+                y[:, lo:hi],
+                t[:, cols],
                 MULT,
             )
 
-        interleave(0, nc.vector.tensor_copy)
-        quantise(0)
-        multiply(0)
-        interleave(1, nc.scalar.copy)
-        quantise(1)
-        multiply(1)
-        interleave(2, nc.scalar.copy)
-        place(0)
-        quantise(2)
-        multiply(2)
-        interleave(3, nc.scalar.copy)
-        place(1)
-        quantise(3)
-        multiply(3)
-        place(2)
-        place(3)
+        interleave(nc.vector.tensor_copy, 0, 128)
+        quantise(0, 128)
+        interleave(nc.vector.tensor_copy, 128, 288)
+        interleave(nc.scalar.copy, 288, 384)
+        interleave(nc.vector.tensor_copy, 384, 416)
+        interleave(nc.scalar.copy, 416, 512)
+        quantise(128, 384)
+        quantise(384, 512)
+        multiply(0, 128)
+        activate(0, 128)
+        multiply(128, 384)
+        multiply(384, 512)
+        activate(128, 384)
+        activate(384, 512)
+        place(0, 128)
+        place(128, 512)
         nc.sync.dma_start(out=out, in_=window[:])

@@ -17,9 +17,12 @@ MULT = mybir.AluOpType.mult
 
 P = 128
 PACK = 4
-BANKS = ((0, 128), (128, 384), (384, 512))
-X_LOADS = ((0, 128), (128, 384), (384, 512))
-GATE_LOADS = ((0, 128), (128, 512))
+GROUP = 16
+
+PIECES = ((0, 128), (128, 384), (384, 512))
+SCALAR_SHARE = (0, 96, 96)
+SCATTERS = ((0, 128), (128, 512))
+CLEARED_BY_SCALAR = 16
 
 
 def tile_picked_place_lin_gelu_sub_l_kernel(tc, xT, w_words, w_scales, b, gate, offs, out):
@@ -28,116 +31,91 @@ def tile_picked_place_lin_gelu_sub_l_kernel(tc, xT, w_words, w_scales, b, gate, 
         keep = ctx.enter_context(tc.tile_pool(name="keep", bufs=1))
         psum = ctx.enter_context(tc.psum_pool(name="psum", bufs=1))
 
-        offsets = keep.tile([P, S // 16], U16, name="offsets")
+        offsets = keep.tile([P, S // GROUP], U16, name="offsets")
         w_codes = keep.tile([P, N], U32, name="w_codes", align_bytes=64)
-        w_plane = keep.tile([P, N], U8, name="w_plane", align_bytes=64)
+        w_scale_tile = keep.tile([P, N], U8, name="w_scale_tile", align_bytes=64)
         bias = keep.tile([P, 1], F32, name="bias")
         window = keep.tile([P, T], F32, name="window", align_bytes=64)
-        warm_in = keep.tile([P, 1], F32, name="warm_in")
-        warm_out = keep.tile([P, 1], F32, name="warm_out")
+        raw = [keep.tile([P, PACK, hi - lo], F32, name=f"raw{lo}", align_bytes=64) for lo, hi in PIECES]
+        gates = [keep.tile([P, hi - lo], F32, name=f"gates{lo}", align_bytes=64) for lo, hi in SCATTERS]
 
-        x_rows = xT.rearrange("(p j) w -> p j w", j=PACK)
-        raw = [keep.tile([P, PACK, hi - lo], F32, name=f"raw{lo}", align_bytes=64) for lo, hi in X_LOADS]
-        gates = [keep.tile([P, hi - lo], F32, name=f"gates{lo}", align_bytes=64) for lo, hi in GATE_LOADS]
-
-        def load_x(queue, k):
-            lo, hi = X_LOADS[k]
-            queue.dma_start(out=raw[k][:], in_=x_rows[:, :, lo:hi])
-
-        def load_gate(queue, k):
-            lo, hi = GATE_LOADS[k]
-            queue.dma_start(out=gates[k][:], in_=gate[:, lo:hi])
-
-        def load_scales(queue, q):
-            queue.dma_start(
-                out=w_plane[32 * q : 32 * q + 4, :].bitcast(I32),
+        x_rows = xT.rearrange("(p t) j -> p t j", t=PACK)
+        for q in range(P // 32):
+            nc.scalar.dma_start(
+                out=w_scale_tile[32 * q : 32 * q + 4, :].bitcast(I32),
                 in_=w_scales[0, 4 * q : 4 * q + 4, :].bitcast(I32),
             )
-
-        def load_w(queue):
-            queue.dma_start(out=w_codes[:].bitcast(I32), in_=w_words[0].rearrange("p n t -> p (n t)").bitcast(I32))
-
-        def held(loads, tiles, lo, hi):
-            for (a, z), t in zip(loads, tiles):
-                if a <= lo and hi <= z:
-                    return t, slice(lo - a, hi - a)
-            raise ValueError("no load holds these columns")
-
-        load_scales(nc.scalar, 0)
-        load_x(nc.sync, 0)
-        load_scales(nc.scalar, 1)
-        load_x(nc.sync, 1)
-        load_scales(nc.scalar, 2)
-        load_x(nc.sync, 2)
-        load_scales(nc.scalar, 3)
-        load_w(nc.sync)
+            if q < len(PIECES):
+                lo, hi = PIECES[q]
+                nc.sync.dma_start(out=raw[q][:], in_=x_rows[:, :, lo:hi])
+        nc.sync.dma_start(out=w_codes[:].bitcast(I32), in_=w_words[0].rearrange("p n t -> p (n t)").bitcast(I32))
         nc.gpsimd.dma_start(out=bias[:], in_=b)
         nc.sync.dma_start(offsets[:], offs)
-        load_gate(nc.sync, 0)
-        load_gate(nc.sync, 1)
-        nc.vector.memset(warm_in[:], 0.0)
-        nc.scalar.activation(warm_out[:], warm_in[:], GELU)
-        nc.vector.memset(window[:], 0.0)
+        for tile, (lo, hi) in zip(gates, SCATTERS):
+            nc.sync.dma_start(out=tile[:], in_=gate[:, lo:hi])
+
+        edge = CLEARED_BY_SCALAR
+        nc.vector.memset(window[:, edge : 2 * edge], 0.0)
+        nc.scalar.activation(window[:, :edge], window[:, edge : 2 * edge], GELU)
+        nc.vector.memset(window[:, 2 * edge :], 0.0)
 
         grouped = keep.tile([P, S * PACK], BF16, name="grouped", align_bytes=64)
-        codes = keep.tile([P, S], U32, name="codes", align_bytes=64)
-        plane = keep.tile([P, S], U8, name="plane", align_bytes=64)
+        x_codes = keep.tile([P, S], U32, name="x_codes", align_bytes=64)
+        x_scale_tile = keep.tile([P, S], U8, name="x_scale_tile", align_bytes=64)
         y = keep.tile([N, S], F32, name="y", align_bytes=64)
-        acc = [psum.tile([N, hi - lo], F32, name=f"acc{lo}") for lo, hi in BANKS]
+        acc = [psum.tile([N, hi - lo], F32, name=f"acc{lo}") for lo, hi in PIECES]
 
-        def interleave(copy, lo, hi):
-            t, cols = held(X_LOADS, raw, lo, hi)
-            copy(
-                out=grouped[:, PACK * lo : PACK * hi].rearrange("p (w j) -> p w j", j=PACK),
-                in_=t[:, :, cols].rearrange("p j w -> p w j"),
-            )
+        def interleave(i):
+            lo, hi = PIECES[i]
+            cut = hi - SCALAR_SHARE[i]
+            for copy, first, last in ((nc.vector.tensor_copy, lo, cut), (nc.scalar.copy, cut, hi)):
+                if first < last:
+                    copy(
+                        out=grouped[:, PACK * first : PACK * last].rearrange("p (j t) -> p j t", t=PACK),
+                        in_=raw[i][:, :, first - lo : last - lo].rearrange("p t j -> p j t"),
+                    )
 
-        def quantise(lo, hi):
+        def quantise(i):
+            lo, hi = PIECES[i]
             nc.vector.quantize_mx(
-                out=codes[:, lo:hi].bitcast(FP8X4),
-                scales=plane[:, lo:hi],
+                out=x_codes[:, lo:hi].bitcast(FP8X4),
+                scales=x_scale_tile[:, lo:hi],
                 in_=grouped[:, PACK * lo : PACK * hi],
             )
 
-        def multiply(lo, hi):
-            t, cols = held(BANKS, acc, lo, hi)
+        def multiply(i):
+            lo, hi = PIECES[i]
             nc.tensor.matmul_mx(
-                out=t[:, cols],
+                out=acc[i][:],
                 lhsT=w_codes[:].bitcast(FP8X4),
-                lhsT_scale=w_plane[:],
-                rhs=codes[:, lo:hi].bitcast(FP8X4),
-                rhs_scale=plane[:, lo:hi],
+                lhsT_scale=w_scale_tile[:],
+                rhs=x_codes[:, lo:hi].bitcast(FP8X4),
+                rhs_scale=x_scale_tile[:, lo:hi],
                 start=True,
                 stop=True,
             )
 
-        def activate(lo, hi):
-            t, cols = held(BANKS, acc, lo, hi)
-            nc.scalar.activation(y[:, lo:hi], t[:, cols], GELU, bias=bias[:])
+        def activate(i):
+            lo, hi = PIECES[i]
+            nc.scalar.activation(y[:, lo:hi], acc[i][:], GELU, bias=bias[:])
 
-        def place(lo, hi):
-            t, cols = held(GATE_LOADS, gates, lo, hi)
+        interleave(0)
+        quantise(0)
+        later = range(1, len(PIECES))
+        for step in (interleave, quantise):
+            for i in later:
+                step(i)
+        multiply(0)
+        activate(0)
+        for step in (multiply, activate):
+            for i in later:
+                step(i)
+
+        for tile, (lo, hi) in zip(gates, SCATTERS):
             nc.vector.tensor_tensor(
-                window[:].indirect(offsets[:, lo // 16 : hi // 16]),
+                window[:].indirect(offsets[:, lo // GROUP : hi // GROUP]),
                 y[:, lo:hi],
-                t[:, cols],
+                tile[:],
                 MULT,
             )
-
-        interleave(nc.vector.tensor_copy, 0, 128)
-        quantise(0, 128)
-        interleave(nc.vector.tensor_copy, 128, 288)
-        interleave(nc.scalar.copy, 288, 384)
-        interleave(nc.vector.tensor_copy, 384, 416)
-        interleave(nc.scalar.copy, 416, 512)
-        quantise(128, 384)
-        quantise(384, 512)
-        multiply(0, 128)
-        activate(0, 128)
-        multiply(128, 384)
-        multiply(384, 512)
-        activate(128, 384)
-        activate(384, 512)
-        place(0, 128)
-        place(128, 512)
         nc.sync.dma_start(out=out, in_=window[:])

@@ -14,15 +14,12 @@ U8 = mybir.dt.uint8
 FP8X4 = mybir.dt.float8_e4m3fn_x4
 GELU = mybir.ActivationFunctionType.Gelu_apprx_tanh
 MULT = mybir.AluOpType.mult
-
 P = 128
 PACK = 4
 GROUP = 16
-
-PIECES = ((0, 128), (128, 384), (384, 512))
-SCALAR_SHARE = (0, 96, 96)
-SCATTERS = ((0, 128), (128, 512))
-CLEARED_BY_SCALAR = 16
+LOADS = ((0,256,),(256,384,),(384,512,),)
+GATES = ((0,128,),(128,512,),)
+BANKS = ((0,128,),(128,384,),(384,512,),)
 
 
 def tile_picked_place_lin_gelu_sub_l_kernel(tc, xT, w_words, w_scales, b, gate, offs, out):
@@ -32,61 +29,44 @@ def tile_picked_place_lin_gelu_sub_l_kernel(tc, xT, w_words, w_scales, b, gate, 
         psum = ctx.enter_context(tc.psum_pool(name="psum", bufs=1))
 
         offsets = keep.tile([P, S // GROUP], U16, name="offsets")
-        w_codes = keep.tile([P, N], U32, name="w_codes", align_bytes=64)
-        w_scale_tile = keep.tile([P, N], U8, name="w_scale_tile", align_bytes=64)
+        w_codes = keep.tile([P, N], U32, name="w_codes", align_bytes=256)
+        w_scale_tile = keep.tile([P, N], U8, name="w_scale_tile", align_bytes=256)
         bias = keep.tile([P, 1], F32, name="bias")
-        window = keep.tile([P, T], F32, name="window", align_bytes=64)
-        raw = [keep.tile([P, PACK, hi - lo], F32, name=f"raw{lo}", align_bytes=64) for lo, hi in PIECES]
-        gates = [keep.tile([P, hi - lo], F32, name=f"gates{lo}", align_bytes=64) for lo, hi in SCATTERS]
-
+        window = keep.tile([P, T], F32, name="window", align_bytes=256)
+        raw = [None if lo == 256 else keep.tile([P, PACK, hi - lo], F32, name=f"raw{lo}", align_bytes=256) for lo, hi in LOADS]
+        gates = [keep.tile([P, hi - lo], F32, name=f"gates{lo}", align_bytes=256) for lo, hi in GATES]
+        grouped = keep.tile([P, S * PACK], BF16, name="grouped", align_bytes=256)
+        x_codes = keep.tile([P, S], U32, name="x_codes", align_bytes=256)
+        x_scale_tile = keep.tile([P, S], U8, name="x_scale_tile", align_bytes=256)
+        acc = [psum.tile([N, hi - lo], F32, name=f"acc{lo}") for lo, hi in BANKS]
+        shared = keep.tile([P, PACK * 128 - 16 + S], F32, name="shared", align_bytes=256)
+        raw[1] = shared[:, : PACK * 128].rearrange("p (t j) -> p t j", t=PACK)
+        y = shared[:, PACK * 128 - 16 :]
         x_rows = xT.rearrange("(p t) j -> p t j", t=PACK)
-        for q in range(P // 32):
-            nc.scalar.dma_start(
-                out=w_scale_tile[32 * q : 32 * q + 4, :].bitcast(I32),
-                in_=w_scales[0, 4 * q : 4 * q + 4, :].bitcast(I32),
-            )
-            if q < len(PIECES):
-                lo, hi = PIECES[q]
-                nc.sync.dma_start(out=raw[q][:], in_=x_rows[:, :, lo:hi])
-        nc.sync.dma_start(out=w_codes[:].bitcast(I32), in_=w_words[0].rearrange("p n t -> p (n t)").bitcast(I32))
-        nc.gpsimd.dma_start(out=bias[:], in_=b)
-        nc.sync.dma_start(offsets[:], offs)
-        for tile, (lo, hi) in zip(gates, SCATTERS):
-            nc.sync.dma_start(out=tile[:], in_=gate[:, lo:hi])
 
-        edge = CLEARED_BY_SCALAR
-        nc.vector.memset(window[:, edge : 2 * edge], 0.0)
-        nc.scalar.activation(window[:, :edge], window[:, edge : 2 * edge], GELU)
-        nc.vector.memset(window[:, 2 * edge :], 0.0)
+        def bank(lo, hi):
+            for tile, (first, last) in zip(acc, BANKS):
+                if first <= lo and hi <= last:
+                    return tile[:, lo - first : hi - first]
 
-        grouped = keep.tile([P, S * PACK], BF16, name="grouped", align_bytes=64)
-        x_codes = keep.tile([P, S], U32, name="x_codes", align_bytes=64)
-        x_scale_tile = keep.tile([P, S], U8, name="x_scale_tile", align_bytes=64)
-        y = keep.tile([N, S], F32, name="y", align_bytes=64)
-        acc = [psum.tile([N, hi - lo], F32, name=f"acc{lo}") for lo, hi in PIECES]
-
-        def interleave(i):
-            lo, hi = PIECES[i]
-            cut = hi - SCALAR_SHARE[i]
-            for copy, first, last in ((nc.vector.tensor_copy, lo, cut), (nc.scalar.copy, cut, hi)):
-                if first < last:
+        def interleave(copy, first, last):
+            for tile, (lo, hi) in zip(raw, LOADS):
+                if lo <= first and last <= hi:
                     copy(
-                        out=grouped[:, PACK * first : PACK * last].rearrange("p (j t) -> p j t", t=PACK),
-                        in_=raw[i][:, :, first - lo : last - lo].rearrange("p t j -> p j t"),
+                        out=grouped[:, PACK * first : PACK * last].rearrange("p (c i t) -> p c t i", i=4, t=PACK),
+                        in_=tile[:, :, first - lo : last - lo].rearrange("p t (c i) -> p c t i", i=4),
                     )
 
-        def quantise(i):
-            lo, hi = PIECES[i]
+        def quantise(lo, hi):
             nc.vector.quantize_mx(
                 out=x_codes[:, lo:hi].bitcast(FP8X4),
                 scales=x_scale_tile[:, lo:hi],
                 in_=grouped[:, PACK * lo : PACK * hi],
             )
 
-        def multiply(i):
-            lo, hi = PIECES[i]
+        def multiply(lo, hi):
             nc.tensor.matmul_mx(
-                out=acc[i][:],
+                out=bank(lo, hi),
                 lhsT=w_codes[:].bitcast(FP8X4),
                 lhsT_scale=w_scale_tile[:],
                 rhs=x_codes[:, lo:hi].bitcast(FP8X4),
@@ -95,27 +75,54 @@ def tile_picked_place_lin_gelu_sub_l_kernel(tc, xT, w_words, w_scales, b, gate, 
                 stop=True,
             )
 
-        def activate(i):
-            lo, hi = PIECES[i]
-            nc.scalar.activation(y[:, lo:hi], acc[i][:], GELU, bias=bias[:])
+        def result(lo, hi):
+            return y[:, lo:hi]
 
-        interleave(0)
-        quantise(0)
-        later = range(1, len(PIECES))
-        for step in (interleave, quantise):
-            for i in later:
-                step(i)
-        multiply(0)
-        activate(0)
-        for step in (multiply, activate):
-            for i in later:
-                step(i)
+        def activate(lo, hi):
+            nc.scalar.activation(result(lo, hi), bank(lo, hi), GELU, bias=bias[:])
 
-        for tile, (lo, hi) in zip(gates, SCATTERS):
-            nc.vector.tensor_tensor(
-                window[:].indirect(offsets[:, lo // GROUP : hi // GROUP]),
-                y[:, lo:hi],
-                tile[:],
-                MULT,
-            )
+        def scatter(lo, hi):
+            for tile, (first, last) in zip(gates, GATES):
+                if first <= lo and hi <= last:
+                    nc.vector.tensor_tensor(
+                        window[:].indirect(offsets[:, lo // GROUP : hi // GROUP]),
+                        result(lo, hi),
+                        tile[:, lo - first : hi - first],
+                        MULT,
+                    )
+
+        nc.sync.dma_start(out=w_codes[:].bitcast(I32), in_=w_words[0].rearrange("p n t -> p (n t)").bitcast(I32))
+        nc.scalar.dma_start(out=w_scale_tile[0 : 4, :].bitcast(I32), in_=w_scales[0, 0 : 4, :].bitcast(I32))
+        nc.sync.dma_start(out=raw[0][:], in_=x_rows[:, :, 0:256])
+        nc.scalar.dma_start(out=w_scale_tile[32 : 36, :].bitcast(I32), in_=w_scales[0, 4 : 8, :].bitcast(I32))
+        nc.sync.dma_start(out=w_scale_tile[96 : 100, :].bitcast(I32), in_=w_scales[0, 12 : 16, :].bitcast(I32))
+        nc.scalar.dma_start(out=w_scale_tile[64 : 68, :].bitcast(I32), in_=w_scales[0, 8 : 12, :].bitcast(I32))
+        nc.sync.dma_start(out=raw[1], in_=x_rows[:, :, 256:384])
+        nc.sync.dma_start(out=raw[2][:], in_=x_rows[:, :, 384:512])
+        nc.gpsimd.dma_start(out=bias[:], in_=b)
+        nc.sync.dma_start(offsets[:], offs)
+        nc.sync.dma_start(out=gates[0][:], in_=gate[:, 0:128])
+        nc.sync.dma_start(out=gates[1][:], in_=gate[:, 128:512])
+        nc.vector.memset(window[:, 16:32], 0.0)
+        nc.scalar.activation(window[:, :16], window[:, 16:32], GELU)
+        nc.vector.memset(window[:, 32:], 0.0)
+        interleave(nc.vector.tensor_copy, 0, 128)
+        interleave(nc.scalar.copy, 176, 256)
+        interleave(nc.vector.tensor_copy, 128, 176)
+        quantise(0, 128)
+        quantise(128, 256)
+        interleave(nc.scalar.copy, 256, 368)
+        interleave(nc.vector.tensor_copy, 368, 384)
+        interleave(nc.vector.tensor_copy, 384, 512)
+        quantise(256, 384)
+        quantise(384, 512)
+        multiply(0, 128)
+        activate(0, 128)
+        multiply(128, 256)
+        multiply(256, 384)
+        multiply(384, 512)
+        activate(128, 384)
+        activate(384, 512)
+        scatter(0, 128)
+        scatter(128, 512)
         nc.sync.dma_start(out=out, in_=window[:])

@@ -14,12 +14,19 @@ U8 = mybir.dt.uint8
 FP8X4 = mybir.dt.float8_e4m3fn_x4
 GELU = mybir.ActivationFunctionType.Gelu_apprx_tanh
 MULT = mybir.AluOpType.mult
+
 P = 128
 PACK = 4
 GROUP = 16
-LOADS = ((0,256,),(256,384,),(384,512,),)
-GATES = ((0,128,),(128,512,),)
-BANKS = ((0,128,),(128,384,),(384,512,),)
+LINE = 4
+ALIGN = 256
+PIECE = 128
+
+FIRST, SECOND, LAST = (0, 256), (256, 384), (384, 512)
+SCALAR_FROM, SCALAR_UP_TO = 176, 352
+BANKS = ((0, 128), (128, 384), (384, 512))
+SCATTERS = ((0, 128), (128, 512))
+CLEARED_BY_SCALAR = 16
 
 
 def tile_picked_place_lin_gelu_sub_l_kernel(tc, xT, w_words, w_scales, b, gate, offs, out):
@@ -29,33 +36,60 @@ def tile_picked_place_lin_gelu_sub_l_kernel(tc, xT, w_words, w_scales, b, gate, 
         psum = ctx.enter_context(tc.psum_pool(name="psum", bufs=1))
 
         offsets = keep.tile([P, S // GROUP], U16, name="offsets")
-        w_codes = keep.tile([P, N], U32, name="w_codes", align_bytes=256)
-        w_scale_tile = keep.tile([P, N], U8, name="w_scale_tile", align_bytes=256)
+        w_codes = keep.tile([P, N], U32, name="w_codes", align_bytes=ALIGN)
+        w_scale_tile = keep.tile([P, N], U8, name="w_scale_tile", align_bytes=ALIGN)
         bias = keep.tile([P, 1], F32, name="bias")
-        window = keep.tile([P, T], F32, name="window", align_bytes=256)
-        raw = [None if lo == 256 else keep.tile([P, PACK, hi - lo], F32, name=f"raw{lo}", align_bytes=256) for lo, hi in LOADS]
-        gates = [keep.tile([P, hi - lo], F32, name=f"gates{lo}", align_bytes=256) for lo, hi in GATES]
-        grouped = keep.tile([P, S * PACK], BF16, name="grouped", align_bytes=256)
-        x_codes = keep.tile([P, S], U32, name="x_codes", align_bytes=256)
-        x_scale_tile = keep.tile([P, S], U8, name="x_scale_tile", align_bytes=256)
-        acc = [psum.tile([N, hi - lo], F32, name=f"acc{lo}") for lo, hi in BANKS]
-        shared = keep.tile([P, PACK * 128 - 16 + S], F32, name="shared", align_bytes=256)
-        raw[1] = shared[:, : PACK * 128].rearrange("p (t j) -> p t j", t=PACK)
-        y = shared[:, PACK * 128 - 16 :]
+        window = keep.tile([P, T], F32, name="window", align_bytes=ALIGN)
+        raw = {
+            (lo, hi): keep.tile([P, PACK, hi - lo], F32, name=f"raw{lo}", align_bytes=ALIGN)[:]
+            for lo, hi in (FIRST, LAST)
+        }
+        gates = [keep.tile([P, hi - lo], F32, name=f"gates{lo}", align_bytes=ALIGN) for lo, hi in SCATTERS]
+        grouped = keep.tile([P, S * PACK], BF16, name="grouped", align_bytes=ALIGN)
+        x_codes = keep.tile([P, S], U32, name="x_codes", align_bytes=ALIGN)
+        x_scale_tile = keep.tile([P, S], U8, name="x_scale_tile", align_bytes=ALIGN)
+        acc = {(lo, hi): psum.tile([N, hi - lo], F32, name=f"acc{lo}") for lo, hi in BANKS}
+
+        loaded = PACK * (SECOND[1] - SECOND[0])
+        y_start = loaded - (SECOND[1] - SCALAR_UP_TO)
+        shared = keep.tile([P, y_start + S], F32, name="shared", align_bytes=ALIGN)
+        raw[SECOND] = shared[:, :loaded].rearrange("p (t j) -> p t j", t=PACK)
+        y = shared[:, y_start:]
+
         x_rows = xT.rearrange("(p t) j -> p t j", t=PACK)
 
-        def bank(lo, hi):
-            for tile, (first, last) in zip(acc, BANKS):
-                if first <= lo and hi <= last:
-                    return tile[:, lo - first : hi - first]
+        def load_x(load):
+            nc.sync.dma_start(out=raw[load], in_=x_rows[:, :, load[0] : load[1]])
 
-        def interleave(copy, first, last):
-            for tile, (lo, hi) in zip(raw, LOADS):
-                if lo <= first and last <= hi:
-                    copy(
-                        out=grouped[:, PACK * first : PACK * last].rearrange("p (c i t) -> p c t i", i=4, t=PACK),
-                        in_=tile[:, :, first - lo : last - lo].rearrange("p t (c i) -> p c t i", i=4),
-                    )
+        def load_scale_rows(queue, q):
+            queue.dma_start(
+                out=w_scale_tile[32 * q : 32 * q + 4, :].bitcast(I32),
+                in_=w_scales[0, 4 * q : 4 * q + 4, :].bitcast(I32),
+            )
+
+        nc.sync.dma_start(out=w_codes[:].bitcast(I32), in_=w_words[0].rearrange("p n t -> p (n t)").bitcast(I32))
+        load_scale_rows(nc.scalar, 0)
+        load_x(FIRST)
+        load_scale_rows(nc.scalar, 1)
+        load_scale_rows(nc.sync, 3)
+        load_scale_rows(nc.scalar, 2)
+        load_x(SECOND)
+        load_x(LAST)
+        nc.gpsimd.dma_start(out=bias[:], in_=b)
+        nc.sync.dma_start(offsets[:], offs)
+        for tile, (lo, hi) in zip(gates, SCATTERS):
+            nc.sync.dma_start(out=tile[:], in_=gate[:, lo:hi])
+
+        edge = CLEARED_BY_SCALAR
+        nc.vector.memset(window[:, edge : 2 * edge], 0.0)
+        nc.scalar.activation(window[:, :edge], window[:, edge : 2 * edge], GELU)
+        nc.vector.memset(window[:, 2 * edge :], 0.0)
+
+        def interleave(copy, load, lo, hi):
+            copy(
+                out=grouped[:, PACK * lo : PACK * hi].rearrange("p (c i t) -> p c t i", i=LINE, t=PACK),
+                in_=raw[load][:, :, lo - load[0] : hi - load[0]].rearrange("p t (c i) -> p c t i", i=LINE),
+            )
 
         def quantise(lo, hi):
             nc.vector.quantize_mx(
@@ -64,65 +98,47 @@ def tile_picked_place_lin_gelu_sub_l_kernel(tc, xT, w_words, w_scales, b, gate, 
                 in_=grouped[:, PACK * lo : PACK * hi],
             )
 
-        def multiply(lo, hi):
-            nc.tensor.matmul_mx(
-                out=bank(lo, hi),
-                lhsT=w_codes[:].bitcast(FP8X4),
-                lhsT_scale=w_scale_tile[:],
-                rhs=x_codes[:, lo:hi].bitcast(FP8X4),
-                rhs_scale=x_scale_tile[:, lo:hi],
-                start=True,
-                stop=True,
+        interleave(nc.vector.tensor_copy, FIRST, FIRST[0], PIECE)
+        interleave(nc.scalar.copy, FIRST, SCALAR_FROM, FIRST[1])
+        interleave(nc.vector.tensor_copy, FIRST, PIECE, SCALAR_FROM)
+        quantise(FIRST[0], PIECE)
+        quantise(PIECE, FIRST[1])
+        interleave(nc.scalar.copy, SECOND, SECOND[0], SCALAR_UP_TO)
+        interleave(nc.vector.tensor_copy, SECOND, SCALAR_UP_TO, SECOND[1])
+        middle = (LAST[0] + LAST[1]) // 2
+        halves = ((LAST[0], middle), (middle, LAST[1]))
+        for lo, hi in halves:
+            interleave(nc.vector.tensor_copy, LAST, lo, hi)
+        quantise(*SECOND)
+        for lo, hi in halves:
+            quantise(lo, hi)
+
+        def multiply(bank):
+            for lo in range(bank[0], bank[1], PIECE):
+                nc.tensor.matmul_mx(
+                    out=acc[bank][:, lo - bank[0] : lo - bank[0] + PIECE],
+                    lhsT=w_codes[:].bitcast(FP8X4),
+                    lhsT_scale=w_scale_tile[:],
+                    rhs=x_codes[:, lo : lo + PIECE].bitcast(FP8X4),
+                    rhs_scale=x_scale_tile[:, lo : lo + PIECE],
+                    start=True,
+                    stop=True,
+                )
+
+        def activate(bank):
+            nc.scalar.activation(y[:, bank[0] : bank[1]], acc[bank][:], GELU, bias=bias[:])
+
+        multiply(BANKS[0])
+        activate(BANKS[0])
+        for step in (multiply, activate):
+            for bank in BANKS[1:]:
+                step(bank)
+
+        for tile, (lo, hi) in zip(gates, SCATTERS):
+            nc.vector.tensor_tensor(
+                window[:].indirect(offsets[:, lo // GROUP : hi // GROUP]),
+                y[:, lo:hi],
+                tile[:],
+                MULT,
             )
-
-        def result(lo, hi):
-            return y[:, lo:hi]
-
-        def activate(lo, hi):
-            nc.scalar.activation(result(lo, hi), bank(lo, hi), GELU, bias=bias[:])
-
-        def scatter(lo, hi):
-            for tile, (first, last) in zip(gates, GATES):
-                if first <= lo and hi <= last:
-                    nc.vector.tensor_tensor(
-                        window[:].indirect(offsets[:, lo // GROUP : hi // GROUP]),
-                        result(lo, hi),
-                        tile[:, lo - first : hi - first],
-                        MULT,
-                    )
-
-        nc.sync.dma_start(out=w_codes[:].bitcast(I32), in_=w_words[0].rearrange("p n t -> p (n t)").bitcast(I32))
-        nc.scalar.dma_start(out=w_scale_tile[0 : 4, :].bitcast(I32), in_=w_scales[0, 0 : 4, :].bitcast(I32))
-        nc.sync.dma_start(out=raw[0][:], in_=x_rows[:, :, 0:256])
-        nc.scalar.dma_start(out=w_scale_tile[32 : 36, :].bitcast(I32), in_=w_scales[0, 4 : 8, :].bitcast(I32))
-        nc.sync.dma_start(out=w_scale_tile[96 : 100, :].bitcast(I32), in_=w_scales[0, 12 : 16, :].bitcast(I32))
-        nc.scalar.dma_start(out=w_scale_tile[64 : 68, :].bitcast(I32), in_=w_scales[0, 8 : 12, :].bitcast(I32))
-        nc.sync.dma_start(out=raw[1], in_=x_rows[:, :, 256:384])
-        nc.sync.dma_start(out=raw[2][:], in_=x_rows[:, :, 384:512])
-        nc.gpsimd.dma_start(out=bias[:], in_=b)
-        nc.sync.dma_start(offsets[:], offs)
-        nc.sync.dma_start(out=gates[0][:], in_=gate[:, 0:128])
-        nc.sync.dma_start(out=gates[1][:], in_=gate[:, 128:512])
-        nc.vector.memset(window[:, 16:32], 0.0)
-        nc.scalar.activation(window[:, :16], window[:, 16:32], GELU)
-        nc.vector.memset(window[:, 32:], 0.0)
-        interleave(nc.vector.tensor_copy, 0, 128)
-        interleave(nc.scalar.copy, 176, 256)
-        interleave(nc.vector.tensor_copy, 128, 176)
-        quantise(0, 128)
-        quantise(128, 256)
-        interleave(nc.scalar.copy, 256, 368)
-        interleave(nc.vector.tensor_copy, 368, 384)
-        interleave(nc.vector.tensor_copy, 384, 512)
-        quantise(256, 384)
-        quantise(384, 512)
-        multiply(0, 128)
-        activate(0, 128)
-        multiply(128, 256)
-        multiply(256, 384)
-        multiply(384, 512)
-        activate(128, 384)
-        activate(384, 512)
-        scatter(0, 128)
-        scatter(128, 512)
         nc.sync.dma_start(out=out, in_=window[:])

@@ -14,19 +14,12 @@ U8 = mybir.dt.uint8
 FP8X4 = mybir.dt.float8_e4m3fn_x4
 GELU = mybir.ActivationFunctionType.Gelu_apprx_tanh
 MULT = mybir.AluOpType.mult
-
 P = 128
 PACK = 4
 GROUP = 16
-LINE = 4
-ALIGN = 256
-PIECE = 128
-
-FIRST, SECOND, LAST = (0, 256), (256, 384), (384, 512)
-SCALAR_FROM, SCALAR_UP_TO = 176, 352
-BANKS = ((0, 128), (128, 384), (384, 512))
-SCATTERS = ((0, 128), (128, 512))
-CLEARED_BY_SCALAR = 16
+LOADS = ((0,256,),(256,384,),(384,512,),)
+GATES = ((0,128,),(128,512,),)
+BANKS = ((0,128,),(128,256,),(256,384,),(384,512,),)
 
 
 def tile_picked_place_lin_gelu_sub_l_kernel(tc, xT, w_words, w_scales, b, gate, offs, out):
@@ -36,60 +29,34 @@ def tile_picked_place_lin_gelu_sub_l_kernel(tc, xT, w_words, w_scales, b, gate, 
         psum = ctx.enter_context(tc.psum_pool(name="psum", bufs=1))
 
         offsets = keep.tile([P, S // GROUP], U16, name="offsets")
-        w_codes = keep.tile([P, N], U32, name="w_codes", align_bytes=ALIGN)
-        w_scale_tile = keep.tile([P, N], U8, name="w_scale_tile", align_bytes=ALIGN)
+        w_codes = keep.tile([P, N], U32, name="w_codes", align_bytes=256)
+        w_scale_tile = keep.tile([P, N], U8, name="w_scale_tile", align_bytes=256)
         bias = keep.tile([P, 1], F32, name="bias")
-        window = keep.tile([P, T], F32, name="window", align_bytes=ALIGN)
-        raw = {
-            (lo, hi): keep.tile([P, PACK, hi - lo], F32, name=f"raw{lo}", align_bytes=ALIGN)[:]
-            for lo, hi in (FIRST, LAST)
-        }
-        gates = [keep.tile([P, hi - lo], F32, name=f"gates{lo}", align_bytes=ALIGN) for lo, hi in SCATTERS]
-        grouped = keep.tile([P, S * PACK], BF16, name="grouped", align_bytes=ALIGN)
-        x_codes = keep.tile([P, S], U32, name="x_codes", align_bytes=ALIGN)
-        x_scale_tile = keep.tile([P, S], U8, name="x_scale_tile", align_bytes=ALIGN)
-        acc = {(lo, hi): psum.tile([N, hi - lo], F32, name=f"acc{lo}") for lo, hi in BANKS}
-
-        loaded = PACK * (SECOND[1] - SECOND[0])
-        y_start = loaded - (SECOND[1] - SCALAR_UP_TO)
-        shared = keep.tile([P, y_start + S], F32, name="shared", align_bytes=ALIGN)
-        raw[SECOND] = shared[:, :loaded].rearrange("p (t j) -> p t j", t=PACK)
-        y = shared[:, y_start:]
-
+        window = keep.tile([P, T], F32, name="window", align_bytes=256)
+        raw = [None if lo == 256 else keep.tile([P, PACK, hi - lo], F32, name=f"raw{lo}", align_bytes=256) for lo, hi in LOADS]
+        gates = [keep.tile([P, hi - lo], F32, name=f"gates{lo}", align_bytes=256) for lo, hi in GATES]
+        grouped = keep.tile([P, S * PACK], BF16, name="grouped", align_bytes=256)
+        x_codes = keep.tile([P, S], U32, name="x_codes", align_bytes=256)
+        x_scale_tile = keep.tile([P, S], U8, name="x_scale_tile", align_bytes=256)
+        acc = [psum.tile([N, hi - lo], F32, name=f"acc{lo}") for lo, hi in BANKS]
+        shared = keep.tile([P, 512 - 32 + 128], F32, name="shared", align_bytes=256)
+        raw[1] = shared[:, :512].rearrange("p (t j) -> p t j", t=PACK)
+        y_first = shared[:, 512 - 32 :]
+        y_rest = shared[:, :384]
         x_rows = xT.rearrange("(p t) j -> p t j", t=PACK)
 
-        def load_x(load):
-            nc.sync.dma_start(out=raw[load], in_=x_rows[:, :, load[0] : load[1]])
+        def bank(lo, hi):
+            for tile, (first, last) in zip(acc, BANKS):
+                if first <= lo and hi <= last:
+                    return tile[:, lo - first : hi - first]
 
-        def load_scale_rows(queue, q):
-            queue.dma_start(
-                out=w_scale_tile[32 * q : 32 * q + 4, :].bitcast(I32),
-                in_=w_scales[0, 4 * q : 4 * q + 4, :].bitcast(I32),
-            )
-
-        nc.sync.dma_start(out=w_codes[:].bitcast(I32), in_=w_words[0].rearrange("p n t -> p (n t)").bitcast(I32))
-        load_scale_rows(nc.scalar, 0)
-        load_x(FIRST)
-        load_scale_rows(nc.scalar, 1)
-        load_scale_rows(nc.sync, 3)
-        load_scale_rows(nc.scalar, 2)
-        load_x(SECOND)
-        load_x(LAST)
-        nc.gpsimd.dma_start(out=bias[:], in_=b)
-        nc.sync.dma_start(offsets[:], offs)
-        for tile, (lo, hi) in zip(gates, SCATTERS):
-            nc.sync.dma_start(out=tile[:], in_=gate[:, lo:hi])
-
-        edge = CLEARED_BY_SCALAR
-        nc.vector.memset(window[:, edge : 2 * edge], 0.0)
-        nc.scalar.activation(window[:, :edge], window[:, edge : 2 * edge], GELU)
-        nc.vector.memset(window[:, 2 * edge :], 0.0)
-
-        def interleave(copy, load, lo, hi):
-            copy(
-                out=grouped[:, PACK * lo : PACK * hi].rearrange("p (c i t) -> p c t i", i=LINE, t=PACK),
-                in_=raw[load][:, :, lo - load[0] : hi - load[0]].rearrange("p t (c i) -> p c t i", i=LINE),
-            )
+        def interleave(copy, first, last):
+            for tile, (lo, hi) in zip(raw, LOADS):
+                if lo <= first and last <= hi:
+                    copy(
+                        out=grouped[:, PACK * first : PACK * last].rearrange("p (c i t) -> p c t i", i=4, t=PACK),
+                        in_=tile[:, :, first - lo : last - lo].rearrange("p t (c i) -> p c t i", i=4),
+                    )
 
         def quantise(lo, hi):
             nc.vector.quantize_mx(
@@ -98,47 +65,68 @@ def tile_picked_place_lin_gelu_sub_l_kernel(tc, xT, w_words, w_scales, b, gate, 
                 in_=grouped[:, PACK * lo : PACK * hi],
             )
 
-        interleave(nc.vector.tensor_copy, FIRST, FIRST[0], PIECE)
-        interleave(nc.scalar.copy, FIRST, SCALAR_FROM, FIRST[1])
-        interleave(nc.vector.tensor_copy, FIRST, PIECE, SCALAR_FROM)
-        quantise(FIRST[0], PIECE)
-        quantise(PIECE, FIRST[1])
-        interleave(nc.scalar.copy, SECOND, SECOND[0], SCALAR_UP_TO)
-        interleave(nc.vector.tensor_copy, SECOND, SCALAR_UP_TO, SECOND[1])
-        middle = (LAST[0] + LAST[1]) // 2
-        halves = ((LAST[0], middle), (middle, LAST[1]))
-        for lo, hi in halves:
-            interleave(nc.vector.tensor_copy, LAST, lo, hi)
-        quantise(*SECOND)
-        for lo, hi in halves:
-            quantise(lo, hi)
-
-        def multiply(bank):
-            for lo in range(bank[0], bank[1], PIECE):
-                nc.tensor.matmul_mx(
-                    out=acc[bank][:, lo - bank[0] : lo - bank[0] + PIECE],
-                    lhsT=w_codes[:].bitcast(FP8X4),
-                    lhsT_scale=w_scale_tile[:],
-                    rhs=x_codes[:, lo : lo + PIECE].bitcast(FP8X4),
-                    rhs_scale=x_scale_tile[:, lo : lo + PIECE],
-                    start=True,
-                    stop=True,
-                )
-
-        def activate(bank):
-            nc.scalar.activation(y[:, bank[0] : bank[1]], acc[bank][:], GELU, bias=bias[:])
-
-        multiply(BANKS[0])
-        activate(BANKS[0])
-        for step in (multiply, activate):
-            for bank in BANKS[1:]:
-                step(bank)
-
-        for tile, (lo, hi) in zip(gates, SCATTERS):
-            nc.vector.tensor_tensor(
-                window[:].indirect(offsets[:, lo // GROUP : hi // GROUP]),
-                y[:, lo:hi],
-                tile[:],
-                MULT,
+        def multiply(lo, hi):
+            nc.tensor.matmul_mx(
+                out=bank(lo, hi),
+                lhsT=w_codes[:].bitcast(FP8X4),
+                lhsT_scale=w_scale_tile[:],
+                rhs=x_codes[:, lo:hi].bitcast(FP8X4),
+                rhs_scale=x_scale_tile[:, lo:hi],
+                start=True,
+                stop=True,
             )
+
+        def result(lo, hi):
+            return y_first if lo == 0 else y_rest[:, lo - 128 : hi - 128]
+
+        def activate(lo, hi):
+            nc.scalar.activation(result(lo, hi), bank(lo, hi), GELU, bias=bias[:])
+
+        def scatter(lo, hi):
+            for tile, (first, last) in zip(gates, GATES):
+                if first <= lo and hi <= last:
+                    nc.vector.tensor_tensor(
+                        window[:].indirect(offsets[:, lo // GROUP : hi // GROUP]),
+                        result(lo, hi),
+                        tile[:, lo - first : hi - first],
+                        MULT,
+                    )
+
+        nc.sync.dma_start(out=w_codes[:].bitcast(I32), in_=w_words[0].rearrange("p n t -> p (n t)").bitcast(I32))
+        nc.scalar.dma_start(out=w_scale_tile[0 : 4, :].bitcast(I32), in_=w_scales[0, 0 : 4, :].bitcast(I32))
+        nc.sync.dma_start(out=raw[0][:], in_=x_rows[:, :, 0:256])
+        nc.scalar.dma_start(out=w_scale_tile[32 : 36, :].bitcast(I32), in_=w_scales[0, 4 : 8, :].bitcast(I32))
+        nc.sync.dma_start(out=w_scale_tile[96 : 100, :].bitcast(I32), in_=w_scales[0, 12 : 16, :].bitcast(I32))
+        nc.scalar.dma_start(out=w_scale_tile[64 : 68, :].bitcast(I32), in_=w_scales[0, 8 : 12, :].bitcast(I32))
+        nc.sync.dma_start(out=raw[1], in_=x_rows[:, :, 256:384])
+        nc.sync.dma_start(out=raw[2][:], in_=x_rows[:, :, 384:512])
+        nc.gpsimd.dma_start(out=bias[:], in_=b)
+        nc.sync.dma_start(offsets[:], offs)
+        nc.sync.dma_start(out=gates[0][:], in_=gate[:, 0:128])
+        nc.sync.dma_start(out=gates[1][:], in_=gate[:, 128:512])
+        nc.vector.memset(window[:, 16:32], 0.0)
+        nc.scalar.activation(window[:, :16], window[:, 16:32], GELU)
+        nc.vector.memset(window[:, 32:], 0.0)
+        interleave(nc.vector.tensor_copy, 0, 128)
+        interleave(nc.scalar.copy, 176, 256)
+        interleave(nc.vector.tensor_copy, 128, 176)
+        quantise(0, 128)
+        quantise(128, 256)
+        interleave(nc.scalar.copy, 256, 352)
+        interleave(nc.vector.tensor_copy, 352, 384)
+        interleave(nc.vector.tensor_copy, 384, 448)
+        interleave(nc.vector.tensor_copy, 448, 512)
+        quantise(256, 384)
+        quantise(384, 448)
+        quantise(448, 512)
+        multiply(0, 128)
+        activate(0, 128)
+        multiply(128, 256)
+        activate(128, 256)
+        multiply(256, 384)
+        multiply(384, 512)
+        activate(256, 384)
+        activate(384, 512)
+        scatter(0, 128)
+        scatter(128, 512)
         nc.sync.dma_start(out=out, in_=window[:])

@@ -17,9 +17,6 @@ MULT = mybir.AluOpType.mult
 P = 128
 PACK = 4
 GROUP = 16
-LOADS = ((0,256,),(256,384,),(384,512,),)
-GATES = ((0,128,),(128,512,),)
-BANKS = ((0,128,),(128,256,),(256,384,),(384,512,),)
 
 
 def tile_picked_place_lin_gelu_sub_l_kernel(tc, xT, w_words, w_scales, b, gate, offs, out):
@@ -33,41 +30,65 @@ def tile_picked_place_lin_gelu_sub_l_kernel(tc, xT, w_words, w_scales, b, gate, 
         w_scale_tile = keep.tile([P, N], U8, name="w_scale_tile", align_bytes=256)
         bias = keep.tile([P, 1], F32, name="bias")
         window = keep.tile([P, T], F32, name="window", align_bytes=256)
-        raw = [None if lo == 256 else keep.tile([P, PACK, hi - lo], F32, name=f"raw{lo}", align_bytes=256) for lo, hi in LOADS]
-        gates = [keep.tile([P, hi - lo], F32, name=f"gates{lo}", align_bytes=256) for lo, hi in GATES]
-        grouped = keep.tile([P, S * PACK], BF16, name="grouped", align_bytes=256)
         x_codes = keep.tile([P, S], U32, name="x_codes", align_bytes=256)
         x_scale_tile = keep.tile([P, S], U8, name="x_scale_tile", align_bytes=256)
-        acc = [psum.tile([N, hi - lo], F32, name=f"acc{lo}") for lo, hi in BANKS]
-        shared = keep.tile([P, 512 - 32 + 128], F32, name="shared", align_bytes=256)
-        raw[1] = shared[:, :512].rearrange("p (t j) -> p t j", t=PACK)
-        y_first = shared[:, 512 - 32 :]
-        y_rest = shared[:, :384]
         x_rows = xT.rearrange("(p t) j -> p t j", t=PACK)
+        x0 = keep.tile([P, PACK, 256], F32, name="x0", align_bytes=256)
+        x2 = keep.tile([P, PACK, 128], F32, name="x2", align_bytes=256)
+        g0 = keep.tile([P, 128], F32, name="g0", align_bytes=256)
+        g1 = keep.tile([P, 384], F32, name="g1", align_bytes=256)
+        whole = keep.tile([P, S * PACK], BF16, name="whole", align_bytes=256)
+        shared = keep.tile([P, 512 - 32 + 128], F32, name="shared", align_bytes=256)
+        raw = [(0, 256, x0[:]), (256, 384, shared[:, :512].rearrange("p (t j) -> p t j", t=PACK)), (384, 512, x2[:])]
+        gates = [(0, 128, g0[:]), (128, 512, g1[:])]
+        banks = [(lo, lo + 128, psum.tile([N, 128], F32, name=f"acc{lo}")) for lo in range(0, S, 128)]
+        results = [(0, 128, shared[:, 512 - 32 :]), (128, 512, shared[:, :384])]
+        grouped = [(0, 512, whole)]
 
-        def bank(lo, hi):
-            for tile, (first, last) in zip(acc, BANKS):
+        def find(tiles, lo, hi):
+            for first, last, tile in tiles:
                 if first <= lo and hi <= last:
-                    return tile[:, lo - first : hi - first]
+                    return first, tile
 
-        def interleave(copy, first, last):
-            for tile, (lo, hi) in zip(raw, LOADS):
-                if lo <= first and last <= hi:
-                    copy(
-                        out=grouped[:, PACK * first : PACK * last].rearrange("p (c i t) -> p c t i", i=4, t=PACK),
-                        in_=tile[:, :, first - lo : last - lo].rearrange("p t (c i) -> p c t i", i=4),
-                    )
+        def cut(tiles, lo, hi):
+            first, tile = find(tiles, lo, hi)
+            return tile[:, lo - first : hi - first]
+
+        def load_x(queue, i):
+            lo, hi, tile = raw[i]
+            queue.dma_start(out=tile, in_=x_rows[:, :, lo:hi])
+
+        def load_gate(queue, i):
+            lo, hi, tile = gates[i]
+            queue.dma_start(out=tile, in_=gate[:, lo:hi])
+
+        def load_scales(queue, q):
+            queue.dma_start(out=w_scale_tile[32 * q : 32 * q + 4, :].bitcast(I32), in_=w_scales[0, 4 * q : 4 * q + 4, :].bitcast(I32))
+
+        def load_w(queue):
+            queue.dma_start(out=w_codes[:].bitcast(I32), in_=w_words[0].rearrange("p n t -> p (n t)").bitcast(I32))
+
+        def rounded(lo, hi):
+            first, tile = find(grouped, lo, hi)
+            return tile[:, PACK * (lo - first) : PACK * (hi - first)]
+
+        def interleave(copy, lo, hi):
+            first, tile = find(raw, lo, hi)
+            copy(
+                out=rounded(lo, hi).rearrange("p (c i t) -> p c t i", i=4, t=PACK),
+                in_=tile[:, :, lo - first : hi - first].rearrange("p t (c i) -> p c t i", i=4),
+            )
 
         def quantise(lo, hi):
             nc.vector.quantize_mx(
                 out=x_codes[:, lo:hi].bitcast(FP8X4),
                 scales=x_scale_tile[:, lo:hi],
-                in_=grouped[:, PACK * lo : PACK * hi],
+                in_=rounded(lo, hi),
             )
 
         def multiply(lo, hi):
             nc.tensor.matmul_mx(
-                out=bank(lo, hi),
+                out=cut(banks, lo, hi),
                 lhsT=w_codes[:].bitcast(FP8X4),
                 lhsT_scale=w_scale_tile[:],
                 rhs=x_codes[:, lo:hi].bitcast(FP8X4),
@@ -76,37 +97,32 @@ def tile_picked_place_lin_gelu_sub_l_kernel(tc, xT, w_words, w_scales, b, gate, 
                 stop=True,
             )
 
-        def result(lo, hi):
-            return y_first if lo == 0 else y_rest[:, lo - 128 : hi - 128]
-
         def activate(lo, hi):
-            nc.scalar.activation(result(lo, hi), bank(lo, hi), GELU, bias=bias[:])
+            nc.scalar.activation(cut(results, lo, hi), cut(banks, lo, hi), GELU, bias=bias[:])
 
         def scatter(lo, hi):
-            for tile, (first, last) in zip(gates, GATES):
-                if first <= lo and hi <= last:
-                    nc.vector.tensor_tensor(
-                        window[:].indirect(offsets[:, lo // GROUP : hi // GROUP]),
-                        result(lo, hi),
-                        tile[:, lo - first : hi - first],
-                        MULT,
-                    )
+            nc.vector.tensor_tensor(
+                window[:].indirect(offsets[:, lo // GROUP : hi // GROUP]),
+                cut(results, lo, hi),
+                cut(gates, lo, hi),
+                MULT,
+            )
 
-        nc.sync.dma_start(out=w_codes[:].bitcast(I32), in_=w_words[0].rearrange("p n t -> p (n t)").bitcast(I32))
-        nc.scalar.dma_start(out=w_scale_tile[0 : 4, :].bitcast(I32), in_=w_scales[0, 0 : 4, :].bitcast(I32))
-        nc.sync.dma_start(out=raw[0][:], in_=x_rows[:, :, 0:256])
-        nc.scalar.dma_start(out=w_scale_tile[32 : 36, :].bitcast(I32), in_=w_scales[0, 4 : 8, :].bitcast(I32))
-        nc.sync.dma_start(out=w_scale_tile[96 : 100, :].bitcast(I32), in_=w_scales[0, 12 : 16, :].bitcast(I32))
-        nc.scalar.dma_start(out=w_scale_tile[64 : 68, :].bitcast(I32), in_=w_scales[0, 8 : 12, :].bitcast(I32))
-        nc.sync.dma_start(out=raw[1], in_=x_rows[:, :, 256:384])
-        nc.sync.dma_start(out=raw[2][:], in_=x_rows[:, :, 384:512])
+        load_w(nc.sync)
+        load_scales(nc.scalar, 0)
+        load_x(nc.sync, 0)
+        load_scales(nc.sync, 1)
+        load_scales(nc.sync, 2)
+        load_scales(nc.sync, 3)
+        load_x(nc.sync, 1)
+        load_x(nc.sync, 2)
         nc.gpsimd.dma_start(out=bias[:], in_=b)
         nc.sync.dma_start(offsets[:], offs)
-        nc.sync.dma_start(out=gates[0][:], in_=gate[:, 0:128])
-        nc.sync.dma_start(out=gates[1][:], in_=gate[:, 128:512])
-        nc.vector.memset(window[:, 16:32], 0.0)
+        load_gate(nc.sync, 0)
+        load_gate(nc.sync, 1)
+        nc.vector.memset(window[:, 16:33], 0.0)
         nc.scalar.activation(window[:, :16], window[:, 16:32], GELU)
-        nc.vector.memset(window[:, 32:], 0.0)
+        nc.vector.memset(window[:, 33:], 0.0)
         interleave(nc.vector.tensor_copy, 0, 128)
         interleave(nc.scalar.copy, 176, 256)
         interleave(nc.vector.tensor_copy, 128, 176)

@@ -13,7 +13,9 @@ U16 = mybir.dt.uint16
 U8 = mybir.dt.uint8
 FP8X4 = mybir.dt.float8_e4m3fn_x4
 GELU = mybir.ActivationFunctionType.Gelu_apprx_tanh
+COPY = mybir.ActivationFunctionType.Copy
 MULT = mybir.AluOpType.mult
+ADD = mybir.AluOpType.add
 P = 128
 PACK = 4
 GROUP = 16
@@ -29,21 +31,12 @@ def tile_picked_place_lin_gelu_sub_l_kernel(tc, xT, w_words, w_scales, b, gate, 
         w_codes = keep.tile([P, N], U32, name="w_codes", align_bytes=256)
         w_scale_tile = keep.tile([P, N], U8, name="w_scale_tile", align_bytes=256)
         bias = keep.tile([P, 1], F32, name="bias")
-        window = keep.tile([P, T], F32, name="window", align_bytes=256)
+        window_v = keep.tile([P, T], F32, name="window_v", align_bytes=256)
+        window_s = keep.tile([P, T], F32, name="window_s", align_bytes=256)
         x_codes = keep.tile([P, S], U32, name="x_codes", align_bytes=256)
         x_scale_tile = keep.tile([P, S], U8, name="x_scale_tile", align_bytes=256)
         x_rows = xT.rearrange("(p t) j -> p t j", t=PACK)
-        x0 = keep.tile([P, PACK, 256], F32, name="x0", align_bytes=256)
-        x2 = keep.tile([P, PACK, 128], F32, name="x2", align_bytes=256)
-        g0 = keep.tile([P, 128], F32, name="g0", align_bytes=256)
-        g1 = keep.tile([P, 384], F32, name="g1", align_bytes=256)
-        whole = keep.tile([P, S * PACK], BF16, name="whole", align_bytes=256)
-        shared = keep.tile([P, 512 - 32 + 128], F32, name="shared", align_bytes=256)
-        raw = [(0, 256, x0[:]), (256, 384, shared[:, :512].rearrange("p (t j) -> p t j", t=PACK)), (384, 512, x2[:])]
-        gates = [(0, 128, g0[:]), (128, 512, g1[:])]
-        banks = [(lo, lo + 128, psum.tile([N, 128], F32, name=f"acc{lo}")) for lo in range(0, S, 128)]
-        results = [(0, 128, shared[:, 512 - 32 :]), (128, 512, shared[:, :384])]
-        grouped = [(0, 512, whole)]
+        rounded = keep.tile([P, S * PACK], BF16, name="rounded", align_bytes=256)
 
         def find(tiles, lo, hi):
             for first, last, tile in tiles:
@@ -68,14 +61,10 @@ def tile_picked_place_lin_gelu_sub_l_kernel(tc, xT, w_words, w_scales, b, gate, 
         def load_w(queue):
             queue.dma_start(out=w_codes[:].bitcast(I32), in_=w_words[0].rearrange("p n t -> p (n t)").bitcast(I32))
 
-        def rounded(lo, hi):
-            first, tile = find(grouped, lo, hi)
-            return tile[:, PACK * (lo - first) : PACK * (hi - first)]
-
         def interleave(copy, lo, hi):
             first, tile = find(raw, lo, hi)
             copy(
-                out=rounded(lo, hi).rearrange("p (c i t) -> p c t i", i=4, t=PACK),
+                out=rounded[:, PACK * lo : PACK * hi].rearrange("p (c i t) -> p c t i", i=4, t=PACK),
                 in_=tile[:, :, lo - first : hi - first].rearrange("p t (c i) -> p c t i", i=4),
             )
 
@@ -83,7 +72,7 @@ def tile_picked_place_lin_gelu_sub_l_kernel(tc, xT, w_words, w_scales, b, gate, 
             nc.vector.quantize_mx(
                 out=x_codes[:, lo:hi].bitcast(FP8X4),
                 scales=x_scale_tile[:, lo:hi],
-                in_=rounded(lo, hi),
+                in_=rounded[:, PACK * lo : PACK * hi],
             )
 
         def multiply(lo, hi):
@@ -100,13 +89,35 @@ def tile_picked_place_lin_gelu_sub_l_kernel(tc, xT, w_words, w_scales, b, gate, 
         def activate(lo, hi):
             nc.scalar.activation(cut(results, lo, hi), cut(banks, lo, hi), GELU, bias=bias[:])
 
-        def scatter(lo, hi):
+        def weigh(lo, hi):
+            nc.vector.tensor_tensor(cut(weighted, lo, hi), cut(results, lo, hi), cut(gates, lo, hi), MULT)
+
+        def scatter_v(lo, hi):
             nc.vector.tensor_tensor(
-                window[:].indirect(offsets[:, lo // GROUP : hi // GROUP]),
+                window_v[:].indirect(offsets[:, lo // GROUP : hi // GROUP]),
                 cut(results, lo, hi),
                 cut(gates, lo, hi),
                 MULT,
             )
+
+        def scatter_s(lo, hi):
+            nc.scalar.activation(window_s[:].indirect(offsets[:, lo // GROUP : hi // GROUP]), cut(weighted, lo, hi), COPY)
+
+        def merge(queue, lo, hi):
+            nc.vector.tensor_tensor(window_v[:, lo:hi], window_v[:, lo:hi], window_s[:, lo:hi], ADD)
+            queue.dma_start(out=out[:, lo:hi], in_=window_v[:, lo:hi])
+
+        x0 = keep.tile([P, PACK, 256], F32, name="x0", align_bytes=256)
+        x2 = keep.tile([P, PACK, 128], F32, name="x2", align_bytes=256)
+        g0 = keep.tile([P, 256], F32, name="g0", align_bytes=256)
+        g1 = keep.tile([P, 256], F32, name="g1", align_bytes=256)
+        shared = keep.tile([P, 512 - 32 + 128], F32, name="shared", align_bytes=256)
+        late = keep.tile([P, 256], F32, name="late", align_bytes=256)
+        raw = [(0, 256, x0[:]), (256, 384, shared[:, :512].rearrange("p (t j) -> p t j", t=PACK)), (384, 512, x2[:])]
+        gates = [(0, 256, g0[:]), (256, 512, g1[:])]
+        banks = [(lo, lo + 128, psum.tile([N, 128], F32, name=f"acc{lo}")) for lo in range(0, S, 128)]
+        results = [(0, 256, shared[:, 512 - 32 - 128 :]), (256, 512, late[:])]
+        weighted = [(0, 256, rounded[:, PACK * 384 :].bitcast(F32))]
 
         load_w(nc.sync)
         load_scales(nc.scalar, 0)
@@ -120,14 +131,15 @@ def tile_picked_place_lin_gelu_sub_l_kernel(tc, xT, w_words, w_scales, b, gate, 
         nc.sync.dma_start(offsets[:], offs)
         load_gate(nc.sync, 0)
         load_gate(nc.sync, 1)
-        nc.vector.memset(window[:, 16:33], 0.0)
-        nc.scalar.activation(window[:, :16], window[:, 16:32], GELU)
-        nc.vector.memset(window[:, 33:], 0.0)
-        interleave(nc.vector.tensor_copy, 0, 128)
-        interleave(nc.scalar.copy, 176, 256)
-        interleave(nc.vector.tensor_copy, 128, 176)
-        quantise(0, 128)
+        nc.vector.memset(window_s[:, 16:33], 0.0)
+        nc.scalar.activation(window_s[:, :16], window_s[:, 16:32], GELU)
+        nc.vector.memset(window_s[:, 33:], 0.0)
+        nc.vector.memset(window_v[:], 0.0)
+        interleave(nc.vector.tensor_copy, 128, 256)
+        interleave(nc.scalar.copy, 48, 128)
+        interleave(nc.vector.tensor_copy, 0, 48)
         quantise(128, 256)
+        quantise(0, 128)
         interleave(nc.scalar.copy, 256, 352)
         interleave(nc.vector.tensor_copy, 352, 384)
         interleave(nc.vector.tensor_copy, 384, 448)
@@ -135,14 +147,11 @@ def tile_picked_place_lin_gelu_sub_l_kernel(tc, xT, w_words, w_scales, b, gate, 
         quantise(256, 384)
         quantise(384, 448)
         quantise(448, 512)
-        multiply(0, 128)
-        activate(0, 128)
-        multiply(128, 256)
-        activate(128, 256)
-        multiply(256, 384)
-        multiply(384, 512)
-        activate(256, 384)
-        activate(384, 512)
-        scatter(0, 128)
-        scatter(128, 512)
-        nc.sync.dma_start(out=out, in_=window[:])
+        for lo in (128, 0, 256, 384):
+            multiply(lo, lo + 128)
+            activate(lo, lo + 128)
+        weigh(0, 256)
+        scatter_s(0, 256)
+        scatter_v(256, 512)
+        for lo in range(0, T, 256):
+            merge(nc.sync, lo, lo + 256)

@@ -109,12 +109,11 @@ def tile_picked_place_lin_gelu_sub_l_kernel(tc, xT, w_words, w_scales, b, gate, 
 
         x0 = keep.tile([P, PACK, 256], F32, name="x0", align_bytes=256)
         x2 = keep.tile([P, PACK, 128], F32, name="x2", align_bytes=256)
-        g0 = keep.tile([P, 256], F32, name="g0", align_bytes=256)
-        g1 = keep.tile([P, 256], F32, name="g1", align_bytes=256)
+        g0 = keep.tile([P, S], F32, name="g0", align_bytes=256)
         shared = keep.tile([P, 512 - 32 + 128], F32, name="shared", align_bytes=256)
         late = keep.tile([P, 256], F32, name="late", align_bytes=256)
         raw = [(0, 256, x0[:]), (256, 384, shared[:, :512].rearrange("p (t j) -> p t j", t=PACK)), (384, 512, x2[:])]
-        gates = [(0, 256, g0[:]), (256, 512, g1[:])]
+        gates = [(0, S, g0[:])]
         banks = [(lo, lo + 128, psum.tile([N, 128], F32, name=f"acc{lo}")) for lo in range(0, S, 128)]
         results = [(0, 256, shared[:, 512 - 32 - 128 :]), (256, 512, late[:])]
         weighted = [(0, 256, rounded[:, PACK * 384 :].bitcast(F32))]
@@ -130,11 +129,11 @@ def tile_picked_place_lin_gelu_sub_l_kernel(tc, xT, w_words, w_scales, b, gate, 
         nc.gpsimd.dma_start(out=bias[:], in_=b)
         nc.sync.dma_start(offsets[:], offs)
         load_gate(nc.sync, 0)
-        load_gate(nc.sync, 1)
         nc.vector.memset(window_s[:, 16:33], 0.0)
         nc.scalar.activation(window_s[:, :16], window_s[:, 16:32], GELU)
         nc.vector.memset(window_s[:, 33:], 0.0)
-        nc.vector.memset(window_v[:], 0.0)
+        nc.vector.memset(window_v[:, :511], 0.0)
+        nc.vector.memset(window_v[:, 511:], 0.0)
         interleave(nc.vector.tensor_copy, 128, 256)
         interleave(nc.scalar.copy, 48, 128)
         interleave(nc.vector.tensor_copy, 0, 48)

@@ -109,14 +109,15 @@ def tile_picked_place_lin_gelu_sub_l_kernel(tc, xT, w_words, w_scales, b, gate, 
 
         x0 = keep.tile([P, PACK, 256], F32, name="x0", align_bytes=256)
         x2 = keep.tile([P, PACK, 128], F32, name="x2", align_bytes=256)
-        g0 = keep.tile([P, S], F32, name="g0", align_bytes=256)
+        g0 = keep.tile([P, 128], F32, name="g0", align_bytes=256)
+        g1 = keep.tile([P, 384], F32, name="g1", align_bytes=256)
         shared = keep.tile([P, 512 - 32 + 128], F32, name="shared", align_bytes=256)
-        late = keep.tile([P, 256], F32, name="late", align_bytes=256)
+        first_weighted = keep.tile([P, 256], F32, name="first_weighted", align_bytes=256)
         raw = [(0, 256, x0[:]), (256, 384, shared[:, :512].rearrange("p (t j) -> p t j", t=PACK)), (384, 512, x2[:])]
-        gates = [(0, S, g0[:])]
+        gates = [(0, 128, g0[:]), (128, 512, g1[:])]
         banks = [(lo, lo + 128, psum.tile([N, 128], F32, name=f"acc{lo}")) for lo in range(0, S, 128)]
-        results = [(0, 256, shared[:, 512 - 32 - 128 :]), (256, 512, late[:])]
-        weighted = [(0, 256, rounded[:, PACK * 384 :].bitcast(F32))]
+        results = [(0, 128, shared[:, 512 - 32 :]), (128, 512, shared[:, :384])]
+        weighted = [(0, 256, first_weighted[:])]
 
         load_w(nc.sync)
         load_scales(nc.scalar, 0)
@@ -129,16 +130,17 @@ def tile_picked_place_lin_gelu_sub_l_kernel(tc, xT, w_words, w_scales, b, gate, 
         nc.gpsimd.dma_start(out=bias[:], in_=b)
         nc.sync.dma_start(offsets[:], offs)
         load_gate(nc.sync, 0)
+        load_gate(nc.sync, 1)
         nc.vector.memset(window_s[:, 16:33], 0.0)
         nc.scalar.activation(window_s[:, :16], window_s[:, 16:32], GELU)
         nc.vector.memset(window_s[:, 33:], 0.0)
         nc.vector.memset(window_v[:, :511], 0.0)
         nc.vector.memset(window_v[:, 511:], 0.0)
-        interleave(nc.vector.tensor_copy, 128, 256)
-        interleave(nc.scalar.copy, 48, 128)
-        interleave(nc.vector.tensor_copy, 0, 48)
-        quantise(128, 256)
+        interleave(nc.vector.tensor_copy, 0, 128)
+        interleave(nc.scalar.copy, 176, 256)
+        interleave(nc.vector.tensor_copy, 128, 176)
         quantise(0, 128)
+        quantise(128, 256)
         interleave(nc.scalar.copy, 256, 352)
         interleave(nc.vector.tensor_copy, 352, 384)
         interleave(nc.vector.tensor_copy, 384, 448)
@@ -146,10 +148,11 @@ def tile_picked_place_lin_gelu_sub_l_kernel(tc, xT, w_words, w_scales, b, gate, 
         quantise(256, 384)
         quantise(384, 448)
         quantise(448, 512)
-        for lo in (128, 0, 256, 384):
+        for lo in range(0, S, 128):
             multiply(lo, lo + 128)
             activate(lo, lo + 128)
-        weigh(0, 256)
+        weigh(0, 128)
+        weigh(128, 256)
         scatter_s(0, 256)
         scatter_v(256, 512)
         for lo in range(0, T, 256):

@@ -109,12 +109,11 @@ def tile_picked_place_lin_gelu_sub_l_kernel(tc, xT, w_words, w_scales, b, gate, 
 
         x0 = keep.tile([P, PACK, 256], F32, name="x0", align_bytes=256)
         x2 = keep.tile([P, PACK, 128], F32, name="x2", align_bytes=256)
-        g0 = keep.tile([P, 128], F32, name="g0", align_bytes=256)
-        g1 = keep.tile([P, 384], F32, name="g1", align_bytes=256)
+        gate_tile = keep.tile([P, S], F32, name="gate_tile", align_bytes=256)
         shared = keep.tile([P, 512 - 32 + 128], F32, name="shared", align_bytes=256)
         first_weighted = keep.tile([P, 256], F32, name="first_weighted", align_bytes=256)
         raw = [(0, 256, x0[:]), (256, 384, shared[:, :512].rearrange("p (t j) -> p t j", t=PACK)), (384, 512, x2[:])]
-        gates = [(0, 128, g0[:]), (128, 512, g1[:])]
+        gates = [(0, S, gate_tile[:])]
         banks = [(lo, lo + 128, psum.tile([N, 128], F32, name=f"acc{lo}")) for lo in range(0, S, 128)]
         results = [(0, 128, shared[:, 512 - 32 :]), (128, 512, shared[:, :384])]
         weighted = [(0, 256, first_weighted[:])]
@@ -122,17 +121,18 @@ def tile_picked_place_lin_gelu_sub_l_kernel(tc, xT, w_words, w_scales, b, gate, 
         load_w(nc.sync)
         load_scales(nc.scalar, 0)
         load_x(nc.sync, 0)
-        load_scales(nc.sync, 1)
-        load_scales(nc.sync, 2)
+        load_scales(nc.scalar, 1)
+        load_scales(nc.scalar, 2)
         load_scales(nc.sync, 3)
         load_x(nc.sync, 1)
         load_x(nc.sync, 2)
-        nc.gpsimd.dma_start(out=bias[:], in_=b)
         nc.sync.dma_start(offsets[:], offs)
-        load_gate(nc.sync, 0)
-        load_gate(nc.sync, 1)
+        nc.sync.dma_start(out=gate_tile[:, :256], in_=gate[:, :256])
+        nc.sync.dma_start(out=gate_tile[:, 256:], in_=gate[:, 256:])
         nc.vector.memset(window_s[:, 16:33], 0.0)
-        nc.scalar.activation(window_s[:, :16], window_s[:, 16:32], GELU)
+        nc.vector.memset(bias[:], 0.0)
+        nc.scalar.activation(window_s[:, :16], window_s[:, 16:32], GELU, bias=bias[:])
+        nc.scalar.dma_start(out=bias[:], in_=b)
         nc.vector.memset(window_s[:, 33:], 0.0)
         nc.vector.memset(window_v[:, :511], 0.0)
         nc.vector.memset(window_v[:, 511:], 0.0)

@@ -126,13 +126,12 @@ def tile_picked_place_lin_gelu_sub_l_kernel(tc, xT, w_words, w_scales, b, gate, 
         load_scales(nc.sync, 3)
         load_x(nc.sync, 1)
         load_x(nc.sync, 2)
-        nc.sync.dma_start(offsets[:], offs)
+        nc.sync.dma_start(out=bias[:], in_=b)
         nc.sync.dma_start(out=gate_tile[:, :256], in_=gate[:, :256])
+        nc.sync.dma_start(offsets[:], offs)
         nc.sync.dma_start(out=gate_tile[:, 256:], in_=gate[:, 256:])
         nc.vector.memset(window_s[:, 16:33], 0.0)
-        nc.vector.memset(bias[:], 0.0)
-        nc.scalar.activation(window_s[:, :16], window_s[:, 16:32], GELU, bias=bias[:])
-        nc.scalar.dma_start(out=bias[:], in_=b)
+        nc.scalar.activation(window_s[:, :16], window_s[:, 16:32], GELU)
         nc.vector.memset(window_s[:, 33:], 0.0)
         nc.vector.memset(window_v[:, :511], 0.0)
         nc.vector.memset(window_v[:, 511:], 0.0)

@@ -92,9 +92,9 @@ def tile_picked_place_lin_gelu_sub_l_kernel(tc, xT, w_words, w_scales, b, gate, 
         def weigh(lo, hi):
             nc.vector.tensor_tensor(cut(weighted, lo, hi), cut(results, lo, hi), cut(gates, lo, hi), MULT)
 
-        def scatter_v(lo, hi):
+        def scatter_v(window, lo, hi):
             nc.vector.tensor_tensor(
-                window_v[:].indirect(offsets[:, lo // GROUP : hi // GROUP]),
+                window[:].indirect(offsets[:, lo // GROUP : hi // GROUP]),
                 cut(results, lo, hi),
                 cut(gates, lo, hi),
                 MULT,
@@ -107,16 +107,17 @@ def tile_picked_place_lin_gelu_sub_l_kernel(tc, xT, w_words, w_scales, b, gate, 
             nc.vector.tensor_tensor(window_v[:, lo:hi], window_v[:, lo:hi], window_s[:, lo:hi], ADD)
             queue.dma_start(out=out[:, lo:hi], in_=window_v[:, lo:hi])
 
-        x0 = keep.tile([P, PACK, 256], F32, name="x0", align_bytes=256)
+        x0 = keep.tile([P, PACK, 192], F32, name="x0", align_bytes=256)
         x2 = keep.tile([P, PACK, 128], F32, name="x2", align_bytes=256)
         gate_tile = keep.tile([P, S], F32, name="gate_tile", align_bytes=256)
-        shared = keep.tile([P, 512 - 32 + 128], F32, name="shared", align_bytes=256)
-        first_weighted = keep.tile([P, 256], F32, name="first_weighted", align_bytes=256)
-        raw = [(0, 256, x0[:]), (256, 384, shared[:, :512].rearrange("p (t j) -> p t j", t=PACK)), (384, 512, x2[:])]
+        shared = keep.tile([P, 768 - 32 + 128], F32, name="shared", align_bytes=256)
+        first_weighted = keep.tile([P, 192], F32, name="first_weighted", align_bytes=256)
+        raw = [(0, 192, x0[:]), (192, 384, shared[:, :768].rearrange("p (t j) -> p t j", t=PACK)), (384, 512, x2[:])]
         gates = [(0, S, gate_tile[:])]
-        banks = [(lo, lo + 128, psum.tile([N, 128], F32, name=f"acc{lo}")) for lo in range(0, S, 128)]
-        results = [(0, 128, shared[:, 512 - 32 :]), (128, 512, shared[:, :384])]
-        weighted = [(0, 256, first_weighted[:])]
+        products = ((0, 128), (128, 192), (320, 384), (192, 320), (384, 512))
+        banks = [(lo, hi, psum.tile([N, hi - lo], F32, name=f"acc{lo}")) for lo, hi in products]
+        results = [(0, 128, shared[:, 768 - 32 :]), (128, 512, shared[:, :384])]
+        weighted = [(128, 320, first_weighted[:])]
 
         load_w(nc.sync)
         load_scales(nc.scalar, 0)
@@ -127,32 +128,33 @@ def tile_picked_place_lin_gelu_sub_l_kernel(tc, xT, w_words, w_scales, b, gate, 
         load_x(nc.sync, 1)
         load_x(nc.sync, 2)
         nc.sync.dma_start(out=bias[:], in_=b)
-        nc.sync.dma_start(out=gate_tile[:, :256], in_=gate[:, :256])
+        nc.sync.dma_start(out=gate_tile[:, :128], in_=gate[:, :128])
         nc.sync.dma_start(offsets[:], offs)
-        nc.sync.dma_start(out=gate_tile[:, 256:], in_=gate[:, 256:])
+        nc.sync.dma_start(out=gate_tile[:, 128:], in_=gate[:, 128:])
         nc.vector.memset(window_s[:, 16:33], 0.0)
         nc.scalar.activation(window_s[:, :16], window_s[:, 16:32], GELU)
         nc.vector.memset(window_s[:, 33:], 0.0)
         nc.vector.memset(window_v[:, :511], 0.0)
         nc.vector.memset(window_v[:, 511:], 0.0)
         interleave(nc.vector.tensor_copy, 0, 128)
-        interleave(nc.scalar.copy, 176, 256)
-        interleave(nc.vector.tensor_copy, 128, 176)
+        interleave(nc.scalar.copy, 128, 192)
         quantise(0, 128)
-        quantise(128, 256)
-        interleave(nc.scalar.copy, 256, 352)
-        interleave(nc.vector.tensor_copy, 352, 384)
+        quantise(128, 192)
+        interleave(nc.scalar.copy, 192, 288)
+        interleave(nc.vector.tensor_copy, 320, 384)
+        interleave(nc.vector.tensor_copy, 288, 320)
+        quantise(320, 384)
         interleave(nc.vector.tensor_copy, 384, 448)
         interleave(nc.vector.tensor_copy, 448, 512)
-        quantise(256, 384)
+        quantise(192, 320)
         quantise(384, 448)
         quantise(448, 512)
-        for lo in range(0, S, 128):
-            multiply(lo, lo + 128)
-            activate(lo, lo + 128)
-        weigh(0, 128)
-        weigh(128, 256)
-        scatter_s(0, 256)
-        scatter_v(256, 512)
+        for lo, hi in products:
+            multiply(lo, hi)
+            activate(lo, hi)
+        scatter_v(window_s, 0, 128)
+        weigh(128, 320)
+        scatter_s(128, 320)
+        scatter_v(window_v, 320, 512)
         for lo in range(0, T, 256):
             merge(nc.sync, lo, lo + 256)

@@ -114,7 +114,7 @@ def tile_picked_place_lin_gelu_sub_l_kernel(tc, xT, w_words, w_scales, b, gate, 
         first_weighted = keep.tile([P, 192], F32, name="first_weighted", align_bytes=256)
         raw = [(0, 192, x0[:]), (192, 384, shared[:, :768].rearrange("p (t j) -> p t j", t=PACK)), (384, 512, x2[:])]
         gates = [(0, S, gate_tile[:])]
-        products = ((0, 128), (128, 192), (320, 384), (192, 320), (384, 512))
+        products = ((0, 128), (128, 192), (192, 320), (320, 384), (384, 512))
         banks = [(lo, hi, psum.tile([N, hi - lo], F32, name=f"acc{lo}")) for lo, hi in products]
         results = [(0, 128, shared[:, 768 - 32 :]), (128, 512, shared[:, :384])]
         weighted = [(128, 320, first_weighted[:])]
@@ -140,13 +140,12 @@ def tile_picked_place_lin_gelu_sub_l_kernel(tc, xT, w_words, w_scales, b, gate, 
         interleave(nc.scalar.copy, 128, 192)
         quantise(0, 128)
         quantise(128, 192)
-        interleave(nc.scalar.copy, 192, 288)
+        interleave(nc.vector.tensor_copy, 192, 320)
         interleave(nc.vector.tensor_copy, 320, 384)
-        interleave(nc.vector.tensor_copy, 288, 320)
-        quantise(320, 384)
         interleave(nc.vector.tensor_copy, 384, 448)
         interleave(nc.vector.tensor_copy, 448, 512)
         quantise(192, 320)
+        quantise(320, 384)
         quantise(384, 448)
         quantise(448, 512)
         for lo, hi in products:

@@ -143,7 +143,7 @@ def tile_picked_place_lin_gelu_sub_l_kernel(tc, xT, w_words, w_scales, b, gate, 
         interleave(nc.vector.tensor_copy, 192, 320)
         interleave(nc.vector.tensor_copy, 320, 384)
         interleave(nc.vector.tensor_copy, 384, 448)
-        interleave(nc.vector.tensor_copy, 448, 512)
+        interleave(nc.scalar.copy, 448, 512)
         quantise(192, 320)
         quantise(320, 384)
         quantise(384, 448)

@@ -137,7 +137,7 @@ def tile_picked_place_lin_gelu_sub_l_kernel(tc, xT, w_words, w_scales, b, gate, 
         nc.vector.memset(window_v[:, :511], 0.0)
         nc.vector.memset(window_v[:, 511:], 0.0)
         interleave(nc.vector.tensor_copy, 0, 128)
-        interleave(nc.scalar.copy, 128, 192)
+        interleave(nc.vector.tensor_copy, 128, 192)
         quantise(0, 128)
         quantise(128, 192)
         interleave(nc.vector.tensor_copy, 192, 320)

@@ -35,8 +35,8 @@ def tile_picked_place_lin_gelu_sub_l_kernel(tc, xT, w_words, w_scales, b, gate, 
         window_s = keep.tile([P, T], F32, name="window_s", align_bytes=256)
         x_codes = keep.tile([P, S], U32, name="x_codes", align_bytes=256)
         x_scale_tile = keep.tile([P, S], U8, name="x_scale_tile", align_bytes=256)
-        x_rows = xT.rearrange("(p t) j -> p t j", t=PACK)
         rounded = keep.tile([P, S * PACK], BF16, name="rounded", align_bytes=256)
+        x_rows = xT.rearrange("(p t) j -> p t j", t=PACK)
 
         def find(tiles, lo, hi):
             for first, last, tile in tiles:
@@ -50,10 +50,6 @@ def tile_picked_place_lin_gelu_sub_l_kernel(tc, xT, w_words, w_scales, b, gate, 
         def load_x(queue, i):
             lo, hi, tile = raw[i]
             queue.dma_start(out=tile, in_=x_rows[:, :, lo:hi])
-
-        def load_gate(queue, i):
-            lo, hi, tile = gates[i]
-            queue.dma_start(out=tile, in_=gate[:, lo:hi])
 
         def load_scales(queue, q):
             queue.dma_start(out=w_scale_tile[32 * q : 32 * q + 4, :].bitcast(I32), in_=w_scales[0, 4 * q : 4 * q + 4, :].bitcast(I32))
@@ -100,24 +96,23 @@ def tile_picked_place_lin_gelu_sub_l_kernel(tc, xT, w_words, w_scales, b, gate, 
                 MULT,
             )
 
-        def scatter_s(lo, hi):
-            nc.scalar.activation(window_s[:].indirect(offsets[:, lo // GROUP : hi // GROUP]), cut(weighted, lo, hi), COPY)
+        def scatter_s(window, lo, hi):
+            nc.scalar.activation(window[:].indirect(offsets[:, lo // GROUP : hi // GROUP]), cut(weighted, lo, hi), COPY)
 
         def merge(queue, lo, hi):
             nc.vector.tensor_tensor(window_v[:, lo:hi], window_v[:, lo:hi], window_s[:, lo:hi], ADD)
             queue.dma_start(out=out[:, lo:hi], in_=window_v[:, lo:hi])
 
         x0 = keep.tile([P, PACK, 192], F32, name="x0", align_bytes=256)
+        x1 = keep.tile([P, PACK, 192], F32, name="x1", align_bytes=256)
         x2 = keep.tile([P, PACK, 128], F32, name="x2", align_bytes=256)
         gate_tile = keep.tile([P, S], F32, name="gate_tile", align_bytes=256)
-        shared = keep.tile([P, 768 - 32 + 128], F32, name="shared", align_bytes=256)
-        first_weighted = keep.tile([P, 192], F32, name="first_weighted", align_bytes=256)
-        raw = [(0, 192, x0[:]), (192, 384, shared[:, :768].rearrange("p (t j) -> p t j", t=PACK)), (384, 512, x2[:])]
+        raw = [(0, 192, x0[:]), (192, 384, x1[:]), (384, 512, x2[:])]
         gates = [(0, S, gate_tile[:])]
         products = ((0, 128), (128, 192), (192, 320), (320, 384), (384, 512))
         banks = [(lo, hi, psum.tile([N, hi - lo], F32, name=f"acc{lo}")) for lo, hi in products]
-        results = [(0, 128, shared[:, 768 - 32 :]), (128, 512, shared[:, :384])]
-        weighted = [(128, 320, first_weighted[:])]
+        results = [(0, S, keep.tile([P, S], F32, name="results", align_bytes=256)[:])]
+        weighted = [(128, 288, keep.tile([P, 160], F32, name="weighted", align_bytes=256)[:])]
 
         load_w(nc.sync)
         load_scales(nc.scalar, 0)
@@ -131,11 +126,9 @@ def tile_picked_place_lin_gelu_sub_l_kernel(tc, xT, w_words, w_scales, b, gate, 
         nc.sync.dma_start(out=gate_tile[:, :128], in_=gate[:, :128])
         nc.sync.dma_start(offsets[:], offs)
         nc.sync.dma_start(out=gate_tile[:, 128:], in_=gate[:, 128:])
-        nc.vector.memset(window_s[:, 16:33], 0.0)
+        nc.vector.memset(window_s[:, 16:], 0.0)
         nc.scalar.activation(window_s[:, :16], window_s[:, 16:32], GELU)
-        nc.vector.memset(window_s[:, 33:], 0.0)
-        nc.vector.memset(window_v[:, :511], 0.0)
-        nc.vector.memset(window_v[:, 511:], 0.0)
+        nc.vector.memset(window_v[:], 0.0)
         interleave(nc.vector.tensor_copy, 0, 128)
         interleave(nc.vector.tensor_copy, 128, 192)
         quantise(0, 128)
@@ -152,8 +145,8 @@ def tile_picked_place_lin_gelu_sub_l_kernel(tc, xT, w_words, w_scales, b, gate, 
             multiply(lo, hi)
             activate(lo, hi)
         scatter_v(window_s, 0, 128)
-        weigh(128, 320)
-        scatter_s(128, 320)
-        scatter_v(window_v, 320, 512)
+        weigh(128, 288)
+        scatter_s(window_s, 128, 288)
+        scatter_v(window_v, 288, 512)
         for lo in range(0, T, 256):
             merge(nc.sync, lo, lo + 256)

@@ -112,7 +112,7 @@ def tile_picked_place_lin_gelu_sub_l_kernel(tc, xT, w_words, w_scales, b, gate, 
         products = ((0, 128), (128, 192), (192, 320), (320, 384), (384, 512))
         banks = [(lo, hi, psum.tile([N, hi - lo], F32, name=f"acc{lo}")) for lo, hi in products]
         results = [(0, S, keep.tile([P, S], F32, name="results", align_bytes=256)[:])]
-        weighted = [(128, 288, keep.tile([P, 160], F32, name="weighted", align_bytes=256)[:])]
+        weighted = [(128, 320, keep.tile([P, 192], F32, name="weighted", align_bytes=256)[:])]
 
         load_w(nc.sync)
         load_scales(nc.scalar, 0)
@@ -135,8 +135,8 @@ def tile_picked_place_lin_gelu_sub_l_kernel(tc, xT, w_words, w_scales, b, gate, 
         quantise(128, 192)
         interleave(nc.vector.tensor_copy, 192, 320)
         interleave(nc.vector.tensor_copy, 320, 384)
-        interleave(nc.vector.tensor_copy, 384, 448)
-        interleave(nc.scalar.copy, 448, 512)
+        interleave(nc.vector.tensor_copy, 384, 464)
+        interleave(nc.scalar.copy, 464, 512)
         quantise(192, 320)
         quantise(320, 384)
         quantise(384, 448)
@@ -145,8 +145,8 @@ def tile_picked_place_lin_gelu_sub_l_kernel(tc, xT, w_words, w_scales, b, gate, 
             multiply(lo, hi)
             activate(lo, hi)
         scatter_v(window_s, 0, 128)
-        weigh(128, 288)
-        scatter_s(window_s, 128, 288)
-        scatter_v(window_v, 288, 512)
+        weigh(128, 320)
+        scatter_s(window_s, 128, 320)
+        scatter_v(window_v, 320, 512)
         for lo in range(0, T, 256):
             merge(nc.sync, lo, lo + 256)

@@ -109,7 +109,7 @@ def tile_picked_place_lin_gelu_sub_l_kernel(tc, xT, w_words, w_scales, b, gate, 
         gate_tile = keep.tile([P, S], F32, name="gate_tile", align_bytes=256)
         raw = [(0, 192, x0[:]), (192, 384, x1[:]), (384, 512, x2[:])]
         gates = [(0, S, gate_tile[:])]
-        products = ((0, 128), (128, 192), (192, 320), (320, 384), (384, 512))
+        products = ((0, 128), (128, 192), (320, 384), (192, 320), (384, 512))
         banks = [(lo, hi, psum.tile([N, hi - lo], F32, name=f"acc{lo}")) for lo, hi in products]
         results = [(0, S, keep.tile([P, S], F32, name="results", align_bytes=256)[:])]
         weighted = [(128, 320, keep.tile([P, 192], F32, name="weighted", align_bytes=256)[:])]
@@ -133,12 +133,13 @@ def tile_picked_place_lin_gelu_sub_l_kernel(tc, xT, w_words, w_scales, b, gate, 
         interleave(nc.vector.tensor_copy, 128, 192)
         quantise(0, 128)
         quantise(128, 192)
-        interleave(nc.vector.tensor_copy, 192, 320)
         interleave(nc.vector.tensor_copy, 320, 384)
+        interleave(nc.vector.tensor_copy, 192, 224)
+        interleave(nc.scalar.copy, 224, 320)
+        quantise(320, 384)
         interleave(nc.vector.tensor_copy, 384, 464)
         interleave(nc.scalar.copy, 464, 512)
         quantise(192, 320)
-        quantise(320, 384)
         quantise(384, 448)
         quantise(448, 512)
         for lo, hi in products:

from contextlib import ExitStack

import concourse.mybir as mybir

K, S, T, N = 512, 512, 1024, 128
FLOPS = 2 * K * S * N

F32 = mybir.dt.float32
BF16 = mybir.dt.bfloat16
I32 = mybir.dt.int32
U32 = mybir.dt.uint32
U16 = mybir.dt.uint16
U8 = mybir.dt.uint8
FP8X4 = mybir.dt.float8_e4m3fn_x4
GELU = mybir.ActivationFunctionType.Gelu_apprx_tanh
COPY = mybir.ActivationFunctionType.Copy
MULT = mybir.AluOpType.mult
ADD = mybir.AluOpType.add
P = 128
PACK = 4
GROUP = 16


def tile_picked_place_lin_gelu_sub_l_kernel(tc, xT, w_words, w_scales, b, gate, offs, out):
    nc = tc.nc
    with ExitStack() as ctx:
        keep = ctx.enter_context(tc.tile_pool(name="keep", bufs=1))
        psum = ctx.enter_context(tc.psum_pool(name="psum", bufs=1))

        offsets = keep.tile([P, S // GROUP], U16, name="offsets")
        w_codes = keep.tile([P, N], U32, name="w_codes", align_bytes=256)
        w_scale_tile = keep.tile([P, N], U8, name="w_scale_tile", align_bytes=256)
        bias = keep.tile([P, 1], F32, name="bias")
        window_v = keep.tile([P, T], F32, name="window_v", align_bytes=256)
        window_s = keep.tile([P, T], F32, name="window_s", align_bytes=256)
        x_codes = keep.tile([P, S], U32, name="x_codes", align_bytes=256)
        x_scale_tile = keep.tile([P, S], U8, name="x_scale_tile", align_bytes=256)
        rounded = keep.tile([P, S * PACK], BF16, name="rounded", align_bytes=256)
        x_rows = xT.rearrange("(p t) j -> p t j", t=PACK)

        def find(tiles, lo, hi):
            for first, last, tile in tiles:
                if first <= lo and hi <= last:
                    return first, tile

        def cut(tiles, lo, hi):
            first, tile = find(tiles, lo, hi)
            return tile[:, lo - first : hi - first]

        def load_x(queue, i):
            lo, hi, tile = raw[i]
            queue.dma_start(out=tile, in_=x_rows[:, :, lo:hi])

        def load_scales(queue, q):
            queue.dma_start(out=w_scale_tile[32 * q : 32 * q + 4, :].bitcast(I32), in_=w_scales[0, 4 * q : 4 * q + 4, :].bitcast(I32))

        def load_w(queue):
            queue.dma_start(out=w_codes[:].bitcast(I32), in_=w_words[0].rearrange("p n t -> p (n t)").bitcast(I32))

        def interleave(copy, lo, hi):
            first, tile = find(raw, lo, hi)
            copy(
                out=rounded[:, PACK * lo : PACK * hi].rearrange("p (c i t) -> p c t i", i=4, t=PACK),
                in_=tile[:, :, lo - first : hi - first].rearrange("p t (c i) -> p c t i", i=4),
            )

        def quantise(lo, hi):
            nc.vector.quantize_mx(
                out=x_codes[:, lo:hi].bitcast(FP8X4),
                scales=x_scale_tile[:, lo:hi],
                in_=rounded[:, PACK * lo : PACK * hi],
            )

        def multiply(lo, hi):
            nc.tensor.matmul_mx(
                out=cut(banks, lo, hi),
                lhsT=w_codes[:].bitcast(FP8X4),
                lhsT_scale=w_scale_tile[:],
                rhs=x_codes[:, lo:hi].bitcast(FP8X4),
                rhs_scale=x_scale_tile[:, lo:hi],
                start=True,
                stop=True,
            )

        def activate(lo, hi):
            nc.scalar.activation(cut(results, lo, hi), cut(banks, lo, hi), GELU, bias=bias[:])

        def weigh(lo, hi):
            nc.vector.tensor_tensor(cut(weighted, lo, hi), cut(results, lo, hi), cut(gates, lo, hi), MULT)

        def scatter_v(window, lo, hi):
            nc.vector.tensor_tensor(
                window[:].indirect(offsets[:, lo // GROUP : hi // GROUP]),
                cut(results, lo, hi),
                cut(gates, lo, hi),
                MULT,
            )

        def scatter_s(window, lo, hi):
            nc.scalar.activation(window[:].indirect(offsets[:, lo // GROUP : hi // GROUP]), cut(weighted, lo, hi), COPY)

        def merge(queue, lo, hi):
            nc.vector.tensor_tensor(window_v[:, lo:hi], window_v[:, lo:hi], window_s[:, lo:hi], ADD)
            queue.dma_start(out=out[:, lo:hi], in_=window_v[:, lo:hi])

        x0 = keep.tile([P, PACK, 192], F32, name="x0", align_bytes=256)
        x1 = keep.tile([P, PACK, 192], F32, name="x1", align_bytes=256)
        x2 = keep.tile([P, PACK, 128], F32, name="x2", align_bytes=256)
        gate_tile = keep.tile([P, S], F32, name="gate_tile", align_bytes=256)
        raw = [(0, 192, x0[:]), (192, 384, x1[:]), (384, 512, x2[:])]
        gates = [(0, S, gate_tile[:])]
        products = ((0, 128), (128, 192), (320, 384), (192, 320), (384, 512))
        banks = [(lo, hi, psum.tile([N, hi - lo], F32, name=f"acc{lo}")) for lo, hi in products]
        results = [(0, S, keep.tile([P, S], F32, name="results", align_bytes=256)[:])]
        weighted = [(128, 320, keep.tile([P, 192], F32, name="weighted", align_bytes=256)[:])]

        load_w(nc.sync)
        load_scales(nc.scalar, 0)
        load_x(nc.sync, 0)
        load_scales(nc.scalar, 1)
        load_scales(nc.scalar, 2)
        load_scales(nc.sync, 3)
        load_x(nc.sync, 1)
        load_x(nc.sync, 2)
        nc.sync.dma_start(out=bias[:], in_=b)
        nc.sync.dma_start(out=gate_tile[:, :128], in_=gate[:, :128])
        nc.sync.dma_start(offsets[:], offs)
        nc.sync.dma_start(out=gate_tile[:, 128:], in_=gate[:, 128:])
        nc.vector.memset(window_s[:, 16:], 0.0)
        nc.scalar.activation(window_s[:, :16], window_s[:, 16:32], GELU)
        nc.vector.memset(window_v[:], 0.0)
        interleave(nc.vector.tensor_copy, 0, 128)
        interleave(nc.vector.tensor_copy, 128, 192)
        quantise(0, 128)
        quantise(128, 192)
        interleave(nc.vector.tensor_copy, 320, 384)
        interleave(nc.vector.tensor_copy, 192, 224)
        interleave(nc.scalar.copy, 224, 320)
        quantise(320, 384)
        interleave(nc.vector.tensor_copy, 384, 464)
        interleave(nc.scalar.copy, 464, 512)
        quantise(192, 320)
        quantise(384, 448)
        quantise(448, 512)
        for lo, hi in products:
            multiply(lo, hi)
            activate(lo, hi)
        scatter_v(window_s, 0, 128)
        weigh(128, 320)
        scatter_s(window_s, 128, 320)
        scatter_v(window_v, 320, 512)
        for lo in range(0, T, 256):
            merge(nc.sync, lo, lo + 256)
